import numpy as np
import ml_dtypes


def mxq(x, axis, fmt="e4m3"):
    dtype, down = {"e4m3": (ml_dtypes.float8_e4m3fn, 7), "e5m2": (ml_dtypes.float8_e5m2, 14)}[fmt]
    v = np.moveaxis(np.asarray(x, np.float32).astype(ml_dtypes.bfloat16).astype(np.float64), axis, -1)
    blocks = v.reshape(v.shape[:-1] + (-1, 32))
    amax = np.abs(blocks).max(-1, keepdims=True)
    byte = np.maximum(np.where(amax > 0, np.frexp(amax)[1] - 1 + 127, 0) - down, 1)
    scale = np.exp2(byte - 127.0)
    codes = (blocks / scale).astype(np.float32).astype(dtype).astype(np.float64)
    return np.moveaxis((codes * scale).reshape(v.shape), -1, axis)


WIDE = False


def mx_kscale(k):
    if not WIDE:
        return np.ones(k)
    levels = np.array([10, -10, 5, -5, 0])
    if k % 512:
        return np.exp2(np.random.permutation(np.resize(levels, k // 32))).repeat(32)
    a = np.empty((k // 512, 16))
    for p in range(k // 512):
        a[p, :8] = np.random.permutation(np.resize(levels, 8))
        for g in range(8):
            far = levels[np.abs(levels - a[p, g]) >= 10]
            a[p, g + 8] = far[np.random.randint(len(far))]
    return np.exp2(a.ravel()).repeat(32)


def f64(x):
    return np.asarray(x).astype(np.float64)


def striped(idx):
    return np.tile(idx.reshape(-1, 16).T, (8, 1)).astype(np.uint16)


def unstriped(offs):
    return offs[:16].T.reshape(-1).astype(np.int64)


def pack_weight(w):
    k, n = w.shape
    w = f64(np.asarray(w, np.float32).astype(ml_dtypes.bfloat16)).reshape(k // 32, 32, n)
    amax = np.abs(w).max(1)
    byte = np.clip(np.where(amax > 0, np.frexp(amax)[1] - 1 + 127 - 7, 1), 1, 254)
    scaled = (w * np.exp2(127.0 - byte)[:, None, :]).reshape(k, n).astype(np.float32)
    words = np.ascontiguousarray(scaled.reshape(k // 512, 128, 4, n).transpose(0, 1, 3, 2)).astype(ml_dtypes.float8_e4m3fn).view(np.uint8)
    return words, np.ascontiguousarray(byte.astype(np.uint8).reshape(k // 512, 16, n))


def unpack_weight(words, scales):
    g, p, n, _ = words.shape
    vals = np.ascontiguousarray(words).view(ml_dtypes.float8_e4m3fn).astype(np.float64) * np.repeat(np.exp2(scales.astype(np.float64) - 127.0), 8, axis=1)[..., None]
    return vals.transpose(0, 1, 3, 2).reshape(g * 512, n)


def gelu(v):
    return 0.5 * v * (1.0 + np.tanh(np.sqrt(2.0 / np.pi) * (v + 0.044715 * v**3)))


K, T, S, V, H, N, J = 512, 2048, 1024, 512, 512, 256, 512


def setup_inputs():
    n = np.random.standard_normal
    s = mx_kscale(K)[:, None]
    u = mx_kscale(H)
    r = mx_kscale(J)[:, None]
    packed_w4 = pack_weight(n((H, N)) / np.sqrt(H) / u[:, None])
    return {
        "xT": (n((K, T)) * s).astype(np.float32),
        "eT": (n((J, V)) * r).astype(np.float32),
        "w1": (n((K, H)) / np.sqrt(3 * K) / s * u).astype(np.float32),
        "w2": (n((K, H)) / np.sqrt(3 * K) / s * u).astype(np.float32),
        "w3": (n((J, H)) / np.sqrt(3 * J) / r * u).astype(np.float32),
        "w4_words": packed_w4[0],
        "w4_scales": packed_w4[1],
        "offs": striped(np.random.permutation(T)[:S]),
    }


def reference(xT, eT, w1, w2, w3, w4_words, w4_scales, offs):
    xq = mxq(f64(xT)[:, unstriped(offs)], 0, "e4m3")
    h = gelu(mxq(f64(w1), 0, "e4m3").T @ xq[:, :V] + mxq(f64(w2), 0, "e4m3").T @ xq[:, V:2 * V] + mxq(f64(w3), 0, "e4m3").T @ mxq(f64(eT), 0, "e4m3"))
    return unpack_weight(w4_words, w4_scales).T @ mxq(h, 0, "e4m3")

@@ -1,0 +1,198 @@
+from contextlib import ExitStack
+
+import concourse.mybir as mybir
+
+K, T, V, H, N = 512, 2048, 512, 512, 256
+FLOPS = 2 * V * (3 * K * H + H * N)
+
+F32 = mybir.dt.float32
+BF16 = mybir.dt.bfloat16
+U32 = mybir.dt.uint32
+I32 = mybir.dt.int32
+U16 = mybir.dt.uint16
+U8 = mybir.dt.uint8
+FP8X4 = mybir.dt.float8_e4m3fn_x4
+GELU = mybir.ActivationFunctionType.Gelu_apprx_tanh
+
+P = 128
+PACK = 4
+CH = 128
+CHUNKS = V // CH
+
+
+def tile_picked_edgeup_gelu_e_kernel(
+    tc, xT, eT, w1, w2, w3, w4_words, w4_scales, offs, out
+):
+    nc = tc.nc
+    with ExitStack() as ctx:
+        keep = ctx.enter_context(tc.tile_pool(name="keep", bufs=1))
+        psum = ctx.enter_context(tc.psum_pool(name="psum", bufs=1))
+
+        def sb(name, shape, dtype):
+            return keep.tile(shape, dtype, name=name, align_bytes=64)
+
+        def copy_on(engine, dst, src):
+            if engine == "vector":
+                nc.vector.tensor_copy(out=dst, in_=src)
+            else:
+                nc.scalar.copy(out=dst, in_=src)
+
+        def quantize(name, src, width):
+            codes = sb(name + "_codes", [P, width], U32)
+            scales = sb(name + "_scales", [P, width], U8)
+            nc.vector.quantize_mx(out=codes[:].bitcast(FP8X4), scales=scales[:], in_=src)
+            return codes, scales
+
+        zero = sb("zero", [P, 1], F32)
+        nc.gpsimd.memset(zero[:], 0.0)
+        gelu_bias = sb("gelu_bias", [P, 1], F32)
+        nc.scalar.activation(out=gelu_bias[:], in_=zero[:], func=GELU)
+
+        w4_sc = sb("w4_sc", [P, N], U8)
+        nc.gpsimd.memset(w4_sc[:].bitcast(I32), 0)
+        for q in range(4):
+            nc.gpsimd.dma_start(
+                out=w4_sc[32 * q : 32 * q + 4, :].bitcast(I32),
+                in_=w4_scales[0, 4 * q : 4 * q + 4, :].bitcast(I32),
+            )
+
+        x_rows = xT.rearrange("(p j) t -> p j t", j=PACK)
+        x_cuts = ((0, 1024, 2048), (0, 1024, 1792, 2048))
+        x_raw = {}
+        offsets = keep.tile([P, 2 * V // 16], U16, name="offsets")
+        for u in range(2):
+            for a, b in zip(x_cuts[u][:-1], x_cuts[u][1:]):
+                x_raw[u, a] = sb("x_raw%d_%d" % (u, a), [P, 2, b - a], F32)
+                nc.sync.dma_start(out=x_raw[u, a][:], in_=x_rows[:, 2 * u : 2 * u + 2, a:b])
+                if u == 0 and a == 0:
+                    nc.sync.dma_start(offsets[:], offs)
+        w_raw = {}
+        for i, w in enumerate((w1, w2, w3)):
+            w_rows = w.rearrange("(p j) c -> p j c", j=PACK)
+            for h in range(2):
+                w_raw[i, h] = sb("w_raw%d_%d" % (i, h), [P, PACK, H // 2], F32)
+                nc.sync.dma_start(out=w_raw[i, h][:], in_=w_rows[:, :, h * H // 2 : (h + 1) * H // 2])
+        e_rows = eT.rearrange("(p j) v -> p j v", j=PACK)
+        e_raw = []
+        w4_cd = sb("w4_cd", [P, N], U32)
+        for c in range(CHUNKS):
+            e_raw.append(sb("e_raw%d" % c, [P, PACK, CH], F32))
+            nc.sync.dma_start(out=e_raw[c][:], in_=e_rows[:, :, c * CH : (c + 1) * CH])
+            if c == 1:
+                nc.sync.dma_start(
+                    out=w4_cd[:].bitcast(I32),
+                    in_=w4_words[0].rearrange("p n r -> p (n r)").bitcast(I32),
+                )
+
+        pairs = [sb("pairs%d" % u, [P, T, 2], BF16) for u in range(2)]
+        picked = [sb("picked%d" % s, [P, V, 2], U32) for s in range(2)]
+
+        def round_pairs(engine, u, start, a, b):
+            copy_on(
+                engine,
+                pairs[u][:, a:b, :],
+                x_raw[u, start][:, :, a - start : b - start].rearrange("p e t -> p t e"),
+            )
+
+        def gather(u):
+            window = pairs[u][:].rearrange("p t e -> p (t e)").bitcast(U32)
+            for s in range(2):
+                nc.vector.tensor_copy(
+                    out=picked[s][:, :, u],
+                    in_=window.indirect(offsets[:, s * V // 16 : (s + 1) * V // 16]),
+                )
+
+        round_pairs("scalar", 0, 0, 0, 1024)
+        round_pairs("vector", 0, 1024, 1024, 1696)
+        round_pairs("scalar", 0, 1024, 1696, 2048)
+        gather(0)
+        round_pairs("scalar", 1, 0, 0, 1024)
+        round_pairs("vector", 1, 1024, 1024, 1792)
+        round_pairs("scalar", 1, 1792, 1792, 2048)
+        gather(1)
+        x_q = [
+            quantize("x%d" % s, picked[s][:].rearrange("p v u -> p (v u)").bitcast(BF16), V)
+            for s in range(2)
+        ]
+
+        w_bf = [sb("w_bf%d" % i, [P, PACK, P, PACK], BF16) for i in range(3)]
+
+        def round_weight(engine, i, m0, m1):
+            h = m0 // 64
+            src = w_raw[i, h][:].rearrange("p j (m t) -> p m j t", t=PACK)
+            copy_on(
+                engine,
+                w_bf[i][:].rearrange("p t m j -> p m j t")[:, m0:m1],
+                src[:, m0 - 64 * h : m1 - 64 * h],
+            )
+
+        def w_flat(i):
+            return w_bf[i][:].rearrange("p t m j -> p (t m j)")
+
+        round_weight("scalar", 0, 0, 64)
+        round_weight("scalar", 0, 64, 128)
+        w_q = {}
+        cd, sc = quantize("w0", w_flat(0), H)
+        for t in range(PACK):
+            w_q[0, t] = (cd[:, t * P : (t + 1) * P], sc[:, t * P : (t + 1) * P])
+        round_weight("scalar", 1, 0, 64)
+        round_weight("vector", 1, 64, 128)
+        cd, sc = quantize("w1", w_flat(1), H)
+        for t in range(PACK):
+            w_q[1, t] = (cd[:, t * P : (t + 1) * P], sc[:, t * P : (t + 1) * P])
+        round_weight("scalar", 2, 0, 64)
+        round_weight("vector", 2, 64, 108)
+        round_weight("scalar", 2, 108, 128)
+        for t in range(PACK):
+            cd, sc = quantize("w2_%d" % t, w_flat(2)[:, t * 512 : (t + 1) * 512], P)
+            w_q[2, t] = (cd[:], sc[:])
+
+        e_q = []
+        for c in range(CHUNKS):
+            e_bf = sb("e_bf%d" % c, [P, CH, PACK], BF16)
+            copy_on(
+                "scalar" if c == 0 else "vector",
+                e_bf[:].rearrange("p (g i) j -> p g j i", i=4),
+                e_raw[c][:].rearrange("p j (g i) -> p g j i", i=4),
+            )
+            e_q.append(quantize("e%d" % c, e_bf[:].rearrange("p v j -> p (v j)"), CH))
+
+        out_rows = out.rearrange("(a p) v -> p a v", p=P)
+        for c in range(CHUNKS):
+            cols = slice(c * CH, (c + 1) * CH)
+            moving = [
+                (x_q[0][0][:, cols], x_q[0][1][:, cols]),
+                (x_q[1][0][:, cols], x_q[1][1][:, cols]),
+                (e_q[c][0][:], e_q[c][1][:]),
+            ]
+            acc = psum.tile([P, PACK, CH], F32, name="acc%d" % c)
+            for t in range(PACK):
+                for i in range(3):
+                    nc.tensor.matmul_mx(
+                        out=acc[:, t, :],
+                        lhsT=w_q[i, t][0].bitcast(FP8X4),
+                        lhsT_scale=w_q[i, t][1],
+                        rhs=moving[i][0].bitcast(FP8X4),
+                        rhs_scale=moving[i][1],
+                        start=(i == 0),
+                        stop=(i == 2),
+                    )
+            h_bf = sb("h_bf%d" % c, [P, CH, PACK], BF16)
+            nc.scalar.activation(
+                out=h_bf[:], in_=acc[:].rearrange("p t v -> p v t"), func=GELU, bias=gelu_bias[:]
+            )
+            h_cd, h_sc = quantize("h%d" % c, h_bf[:].rearrange("p v j -> p (v j)"), CH)
+            res = psum.tile([P, 2, CH], F32, name="res%d" % c)
+            for a in range(2):
+                nc.tensor.matmul_mx(
+                    out=res[:, a, :],
+                    lhsT=w4_cd[:, a * P : (a + 1) * P].bitcast(FP8X4),
+                    lhsT_scale=w4_sc[:, a * P : (a + 1) * P],
+                    rhs=h_cd[:].bitcast(FP8X4),
+                    rhs_scale=h_sc[:],
+                    start=True,
+                    stop=True,
+                )
+            res_sb = sb("res_sb%d" % c, [P, 2, CH], F32)
+            nc.vector.tensor_copy(out=res_sb[:], in_=res[:])
+            nc.sync.dma_start(out=out_rows[:, :, cols], in_=res_sb[:])

@@ -28,8 +28,8 @@ def tile_picked_edgeup_gelu_e_kernel(
         keep = ctx.enter_context(tc.tile_pool(name="keep", bufs=1))
         psum = ctx.enter_context(tc.psum_pool(name="psum", bufs=1))
 
-        def sb(name, shape, dtype):
-            return keep.tile(shape, dtype, name=name, align_bytes=64)
+        def sb(name, shape, dtype, tag=None):
+            return keep.tile(shape, dtype, name=name, tag=tag or name, align_bytes=64)
 
         def copy_on(engine, dst, src):
             if engine == "vector":
@@ -44,20 +44,20 @@ def tile_picked_edgeup_gelu_e_kernel(
             return codes, scales
 
         zero = sb("zero", [P, 1], F32)
-        nc.gpsimd.memset(zero[:], 0.0)
+        nc.vector.memset(zero[:], 0.0)
         gelu_bias = sb("gelu_bias", [P, 1], F32)
         nc.scalar.activation(out=gelu_bias[:], in_=zero[:], func=GELU)
 
         w4_sc = sb("w4_sc", [P, N], U8)
-        nc.gpsimd.memset(w4_sc[:].bitcast(I32), 0)
+        nc.vector.memset(w4_sc[:].bitcast(I32), 0)
         for q in range(4):
-            nc.gpsimd.dma_start(
+            nc.scalar.dma_start(
                 out=w4_sc[32 * q : 32 * q + 4, :].bitcast(I32),
                 in_=w4_scales[0, 4 * q : 4 * q + 4, :].bitcast(I32),
             )
 
         x_rows = xT.rearrange("(p j) t -> p j t", j=PACK)
-        x_cuts = ((0, 1024, 2048), (0, 1024, 1792, 2048))
+        x_cuts = ((0, 1536, 2048), (0, 1024, 1792, 2048))
         x_raw = {}
         offsets = keep.tile([P, 2 * V // 16], U16, name="offsets")
         for u in range(2):
@@ -66,23 +66,37 @@ def tile_picked_edgeup_gelu_e_kernel(
                 nc.sync.dma_start(out=x_raw[u, a][:], in_=x_rows[:, 2 * u : 2 * u + 2, a:b])
                 if u == 0 and a == 0:
                     nc.sync.dma_start(offsets[:], offs)
+        w_cuts = ((0, 64, 128), (0, 64, 128), (0, 64, 96, 128))
         w_raw = {}
-        for i, w in enumerate((w1, w2, w3)):
-            w_rows = w.rearrange("(p j) c -> p j c", j=PACK)
-            for h in range(2):
-                w_raw[i, h] = sb("w_raw%d_%d" % (i, h), [P, PACK, H // 2], F32)
-                nc.sync.dma_start(out=w_raw[i, h][:], in_=w_rows[:, :, h * H // 2 : (h + 1) * H // 2])
+        e_raw = {}
         e_rows = eT.rearrange("(p j) v -> p j v", j=PACK)
-        e_raw = []
         w4_cd = sb("w4_cd", [P, N], U32)
-        for c in range(CHUNKS):
-            e_raw.append(sb("e_raw%d" % c, [P, PACK, CH], F32))
+
+        def load_weight(i, piece):
+            m0, m1 = w_cuts[i][piece], w_cuts[i][piece + 1]
+            w_rows = (w1, w2, w3)[i].rearrange("(p j) c -> p j c", j=PACK)
+            w_raw[i, m0] = sb("w_raw%d_%d" % (i, m0), [P, PACK, PACK * (m1 - m0)], F32)
+            nc.sync.dma_start(out=w_raw[i, m0][:], in_=w_rows[:, :, PACK * m0 : PACK * m1])
+
+        def load_edges(c):
+            e_raw[c] = sb("e_raw%d" % c, [P, PACK, CH], F32)
             nc.sync.dma_start(out=e_raw[c][:], in_=e_rows[:, :, c * CH : (c + 1) * CH])
-            if c == 1:
-                nc.sync.dma_start(
-                    out=w4_cd[:].bitcast(I32),
-                    in_=w4_words[0].rearrange("p n r -> p (n r)").bitcast(I32),
-                )
+
+        load_weight(0, 0)
+        load_weight(0, 1)
+        load_weight(1, 0)
+        load_weight(1, 1)
+        load_weight(2, 0)
+        load_edges(0)
+        load_weight(2, 1)
+        load_weight(2, 2)
+        load_edges(1)
+        load_edges(2)
+        load_edges(3)
+        nc.sync.dma_start(
+            out=w4_cd[:].bitcast(I32),
+            in_=w4_words[0].rearrange("p n r -> p (n r)").bitcast(I32),
+        )
 
         pairs = [sb("pairs%d" % u, [P, T, 2], BF16) for u in range(2)]
         picked = [sb("picked%d" % s, [P, V, 2], U32) for s in range(2)]
@@ -102,13 +116,15 @@ def tile_picked_edgeup_gelu_e_kernel(
                     in_=window.indirect(offsets[:, s * V // 16 : (s + 1) * V // 16]),
                 )
 
-        round_pairs("scalar", 0, 0, 0, 1024)
-        round_pairs("vector", 0, 1024, 1024, 1696)
-        round_pairs("scalar", 0, 1024, 1696, 2048)
+        round_pairs("vector", 0, 0, 0, 1024)
+        round_pairs("scalar", 0, 0, 1024, 1536)
+        round_pairs("vector", 0, 1536, 1536, 1888)
+        round_pairs("scalar", 0, 1536, 1888, 2048)
         gather(0)
         round_pairs("scalar", 1, 0, 0, 1024)
         round_pairs("vector", 1, 1024, 1024, 1792)
-        round_pairs("scalar", 1, 1792, 1792, 2048)
+        round_pairs("vector", 1, 1792, 1792, 1920)
+        round_pairs("scalar", 1, 1792, 1920, 2048)
         gather(1)
         x_q = [
             quantize("x%d" % s, picked[s][:].rearrange("p v u -> p (v u)").bitcast(BF16), V)
@@ -117,82 +133,136 @@ def tile_picked_edgeup_gelu_e_kernel(
 
         w_bf = [sb("w_bf%d" % i, [P, PACK, P, PACK], BF16) for i in range(3)]
 
-        def round_weight(engine, i, m0, m1):
-            h = m0 // 64
-            src = w_raw[i, h][:].rearrange("p j (m t) -> p m j t", t=PACK)
+        def round_weight(engine, i, start, m0, m1):
+            src = w_raw[i, start][:].rearrange("p j (m t) -> p m j t", t=PACK)
             copy_on(
                 engine,
                 w_bf[i][:].rearrange("p t m j -> p m j t")[:, m0:m1],
-                src[:, m0 - 64 * h : m1 - 64 * h],
+                src[:, m0 - start : m1 - start],
             )
 
         def w_flat(i):
             return w_bf[i][:].rearrange("p t m j -> p (t m j)")
 
-        round_weight("scalar", 0, 0, 64)
-        round_weight("scalar", 0, 64, 128)
+        warm = psum.tile([P, V], F32, name="warm", tag="spare")
+
+        def warm_up(stationary, moving, width):
+            nc.tensor.matmul_mx(
+                out=warm[:, 0:width],
+                lhsT=stationary[0][:, 0:P].bitcast(FP8X4),
+                lhsT_scale=stationary[1][:, 0:P],
+                rhs=moving[0][:, 0:width].bitcast(FP8X4),
+                rhs_scale=moving[1][:, 0:width],
+                start=True,
+                stop=True,
+            )
+
+        e_bf = [sb("e_bf%d" % c, [P, CH, PACK], BF16) for c in range(CHUNKS)]
+        e_q = {}
+
+        def round_edges(engine, c):
+            copy_on(
+                engine,
+                e_bf[c][:].rearrange("p (g i) j -> p g j i", i=4),
+                e_raw[c][:].rearrange("p j (g i) -> p g j i", i=4),
+            )
+
+        def quantize_edges(c):
+            e_q[c] = quantize("e%d" % c, e_bf[c][:].rearrange("p v j -> p (v j)"), CH)
+
+        warm_up(x_q[1], x_q[1], V)
+        round_weight("scalar", 0, 0, 0, 64)
+        round_weight("scalar", 0, 64, 64, 128)
         w_q = {}
         cd, sc = quantize("w0", w_flat(0), H)
         for t in range(PACK):
             w_q[0, t] = (cd[:, t * P : (t + 1) * P], sc[:, t * P : (t + 1) * P])
-        round_weight("scalar", 1, 0, 64)
-        round_weight("vector", 1, 64, 128)
+        round_weight("scalar", 1, 0, 0, 64)
+        round_weight("scalar", 1, 64, 64, 128)
+        round_weight("vector", 2, 0, 0, 64)
         cd, sc = quantize("w1", w_flat(1), H)
         for t in range(PACK):
             w_q[1, t] = (cd[:, t * P : (t + 1) * P], sc[:, t * P : (t + 1) * P])
-        round_weight("scalar", 2, 0, 64)
-        round_weight("vector", 2, 64, 108)
-        round_weight("scalar", 2, 108, 128)
-        for t in range(PACK):
-            cd, sc = quantize("w2_%d" % t, w_flat(2)[:, t * 512 : (t + 1) * 512], P)
-            w_q[2, t] = (cd[:], sc[:])
+        warm_up((cd, sc), x_q[1], V)
+        round_edges("scalar", 0)
+        round_weight("vector", 2, 64, 64, 96)
+        quantize_edges(0)
+        warm_up(e_q[0], x_q[1], V)
+        round_weight("vector", 2, 96, 96, 116)
+        round_weight("scalar", 2, 96, 116, 128)
+        for half in range(2):
+            cd, sc = quantize("w2_%d" % half, w_flat(2)[:, half * 1024 : (half + 1) * 1024], 2 * P)
+            for t in range(2):
+                w_q[2, 2 * half + t] = (cd[:, t * P : (t + 1) * P], sc[:, t * P : (t + 1) * P])
+        for c in (1, 2, 3):
+            round_edges("vector" if c == 3 else "scalar", c)
+            quantize_edges(c)
 
-        e_q = []
-        for c in range(CHUNKS):
-            e_bf = sb("e_bf%d" % c, [P, CH, PACK], BF16)
-            copy_on(
-                "scalar" if c == 0 else "vector",
-                e_bf[:].rearrange("p (g i) j -> p g j i", i=4),
-                e_raw[c][:].rearrange("p j (g i) -> p g j i", i=4),
-            )
-            e_q.append(quantize("e%d" % c, e_bf[:].rearrange("p v j -> p (v j)"), CH))
-
-        out_rows = out.rearrange("(a p) v -> p a v", p=P)
-        for c in range(CHUNKS):
+        def first_layer(c, t, dst):
             cols = slice(c * CH, (c + 1) * CH)
             moving = [
                 (x_q[0][0][:, cols], x_q[0][1][:, cols]),
                 (x_q[1][0][:, cols], x_q[1][1][:, cols]),
                 (e_q[c][0][:], e_q[c][1][:]),
             ]
-            acc = psum.tile([P, PACK, CH], F32, name="acc%d" % c)
-            for t in range(PACK):
-                for i in range(3):
-                    nc.tensor.matmul_mx(
-                        out=acc[:, t, :],
-                        lhsT=w_q[i, t][0].bitcast(FP8X4),
-                        lhsT_scale=w_q[i, t][1],
-                        rhs=moving[i][0].bitcast(FP8X4),
-                        rhs_scale=moving[i][1],
-                        start=(i == 0),
-                        stop=(i == 2),
-                    )
-            h_bf = sb("h_bf%d" % c, [P, CH, PACK], BF16)
-            nc.scalar.activation(
-                out=h_bf[:], in_=acc[:].rearrange("p t v -> p v t"), func=GELU, bias=gelu_bias[:]
-            )
-            h_cd, h_sc = quantize("h%d" % c, h_bf[:].rearrange("p v j -> p (v j)"), CH)
-            res = psum.tile([P, 2, CH], F32, name="res%d" % c)
-            for a in range(2):
+            for i in range(3):
                 nc.tensor.matmul_mx(
-                    out=res[:, a, :],
-                    lhsT=w4_cd[:, a * P : (a + 1) * P].bitcast(FP8X4),
-                    lhsT_scale=w4_sc[:, a * P : (a + 1) * P],
-                    rhs=h_cd[:].bitcast(FP8X4),
-                    rhs_scale=h_sc[:],
-                    start=True,
-                    stop=True,
+                    out=dst,
+                    lhsT=w_q[i, t][0].bitcast(FP8X4),
+                    lhsT_scale=w_q[i, t][1],
+                    rhs=moving[i][0].bitcast(FP8X4),
+                    rhs_scale=moving[i][1],
+                    start=(i == 0),
+                    stop=(i == 2),
                 )
+
+        h_q = []
+        for c in range(CHUNKS):
+            h_bf = sb("h_bf%d" % c, [P, CH, PACK], BF16)
+            if c == 0:
+                h_planes = sb("h_planes", [P, PACK, CH], BF16, tag="e_raw2")
+                for t in range(PACK):
+                    acc_t = psum.tile([P, CH], F32, name="acc0_%d" % t, tag="bank%d" % t)
+                    first_layer(c, t, acc_t[:])
+                    nc.scalar.activation(out=h_planes[:, t, :], in_=acc_t[:], func=GELU, bias=gelu_bias[:])
+                nc.vector.tensor_copy(
+                    out=h_bf[:].rearrange("p (g i) t -> p g t i", i=4),
+                    in_=h_planes[:].rearrange("p t (g i) -> p g t i", i=4),
+                )
+            else:
+                acc = psum.tile([P, PACK, CH], F32, name="acc%d" % c)
+                for t in range(PACK):
+                    first_layer(c, t, acc[:, t, :])
+                nc.scalar.activation(
+                    out=h_bf[:], in_=acc[:].rearrange("p t v -> p v t"), func=GELU, bias=gelu_bias[:]
+                )
+            h_q.append(quantize("h%d" % c, h_bf[:].rearrange("p v j -> p (v j)"), CH))
+
+        def second_layer(c, a, dst):
+            nc.tensor.matmul_mx(
+                out=dst,
+                lhsT=w4_cd[:, a * P : (a + 1) * P].bitcast(FP8X4),
+                lhsT_scale=w4_sc[:, a * P : (a + 1) * P],
+                rhs=h_q[c][0][:].bitcast(FP8X4),
+                rhs_scale=h_q[c][1][:],
+                start=True,
+                stop=True,
+            )
+
+        out_rows = out.rearrange("(a p) v -> p a v", p=P)
+        for c in range(CHUNKS - 1):
+            cols = slice(c * CH, (c + 1) * CH)
+            res = psum.tile([P, 2, CH], F32, name="res%d" % c, tag=("spare", "bank0", "bank1")[c])
+            for a in range(2):
+                second_layer(c, a, res[:, a, :])
             res_sb = sb("res_sb%d" % c, [P, 2, CH], F32)
-            nc.vector.tensor_copy(out=res_sb[:], in_=res[:])
+            copy_on("vector" if c == 0 else "scalar", res_sb[:], res[:])
             nc.sync.dma_start(out=out_rows[:, :, cols], in_=res_sb[:])
+        c = CHUNKS - 1
+        cols = slice(c * CH, (c + 1) * CH)
+        for a in range(2):
+            res = psum.tile([P, CH], F32, name="res_last%d" % a, tag="bank%d" % (2 + a))
+            second_layer(c, a, res[:])
+            res_sb = sb("res_last_sb%d" % a, [P, CH], F32)
+            copy_on(("vector", "scalar")[a], res_sb[:], res[:])
+            (nc.sync, nc.scalar)[a].dma_start(out=out_rows[:, a, cols], in_=res_sb[:])

@@ -66,7 +66,7 @@ def tile_picked_edgeup_gelu_e_kernel(
                 nc.sync.dma_start(out=x_raw[u, a][:], in_=x_rows[:, 2 * u : 2 * u + 2, a:b])
                 if u == 0 and a == 0:
                     nc.sync.dma_start(offsets[:], offs)
-        w_cuts = ((0, 64, 128), (0, 64, 128), (0, 64, 96, 128))
+        w_cuts = ((0, 128), (0, 128), (0, 128))
         w_raw = {}
         e_raw = {}
         e_rows = eT.rearrange("(p j) v -> p j v", j=PACK)
@@ -83,13 +83,9 @@ def tile_picked_edgeup_gelu_e_kernel(
             nc.sync.dma_start(out=e_raw[c][:], in_=e_rows[:, :, c * CH : (c + 1) * CH])
 
         load_weight(0, 0)
-        load_weight(0, 1)
         load_weight(1, 0)
-        load_weight(1, 1)
         load_weight(2, 0)
         load_edges(0)
-        load_weight(2, 1)
-        load_weight(2, 2)
         load_edges(1)
         load_edges(2)
         load_edges(3)
@@ -171,31 +167,30 @@ def tile_picked_edgeup_gelu_e_kernel(
             e_q[c] = quantize("e%d" % c, e_bf[c][:].rearrange("p v j -> p (v j)"), CH)
 
         warm_up(x_q[1], x_q[1], V)
-        round_weight("scalar", 0, 0, 0, 64)
-        round_weight("scalar", 0, 64, 64, 128)
+        round_weight("scalar", 0, 0, 0, 128)
         w_q = {}
         cd, sc = quantize("w0", w_flat(0), H)
         for t in range(PACK):
             w_q[0, t] = (cd[:, t * P : (t + 1) * P], sc[:, t * P : (t + 1) * P])
-        round_weight("scalar", 1, 0, 0, 64)
-        round_weight("scalar", 1, 64, 64, 128)
-        round_weight("vector", 2, 0, 0, 64)
+        warm_up((cd, sc), x_q[0], V)
+        round_weight("scalar", 1, 0, 0, 76)
+        round_weight("vector", 1, 0, 76, 128)
         cd, sc = quantize("w1", w_flat(1), H)
         for t in range(PACK):
             w_q[1, t] = (cd[:, t * P : (t + 1) * P], sc[:, t * P : (t + 1) * P])
         warm_up((cd, sc), x_q[1], V)
-        round_edges("scalar", 0)
-        round_weight("vector", 2, 64, 64, 96)
-        quantize_edges(0)
-        warm_up(e_q[0], x_q[1], V)
-        round_weight("vector", 2, 96, 96, 116)
-        round_weight("scalar", 2, 96, 116, 128)
+        round_weight("scalar", 2, 0, 0, 58)
+        round_weight("vector", 2, 0, 58, 128)
+        round_edges("vector", 0)
         for half in range(2):
             cd, sc = quantize("w2_%d" % half, w_flat(2)[:, half * 1024 : (half + 1) * 1024], 2 * P)
             for t in range(2):
                 w_q[2, 2 * half + t] = (cd[:, t * P : (t + 1) * P], sc[:, t * P : (t + 1) * P])
+            if half == 0:
+                warm_up((cd, sc), x_q[1], V // 2)
+                quantize_edges(0)
         for c in (1, 2, 3):
-            round_edges("vector" if c == 3 else "scalar", c)
+            round_edges("scalar" if c == 1 else "vector", c)
             quantize_edges(c)
 
         def first_layer(c, t, dst):
@@ -219,23 +214,12 @@ def tile_picked_edgeup_gelu_e_kernel(
         h_q = []
         for c in range(CHUNKS):
             h_bf = sb("h_bf%d" % c, [P, CH, PACK], BF16)
-            if c == 0:
-                h_planes = sb("h_planes", [P, PACK, CH], BF16, tag="e_raw2")
-                for t in range(PACK):
-                    acc_t = psum.tile([P, CH], F32, name="acc0_%d" % t, tag="bank%d" % t)
-                    first_layer(c, t, acc_t[:])
-                    nc.scalar.activation(out=h_planes[:, t, :], in_=acc_t[:], func=GELU, bias=gelu_bias[:])
-                nc.vector.tensor_copy(
-                    out=h_bf[:].rearrange("p (g i) t -> p g t i", i=4),
-                    in_=h_planes[:].rearrange("p t (g i) -> p g t i", i=4),
-                )
-            else:
-                acc = psum.tile([P, PACK, CH], F32, name="acc%d" % c)
-                for t in range(PACK):
-                    first_layer(c, t, acc[:, t, :])
-                nc.scalar.activation(
-                    out=h_bf[:], in_=acc[:].rearrange("p t v -> p v t"), func=GELU, bias=gelu_bias[:]
-                )
+            acc = psum.tile([P, PACK, CH], F32, name="acc%d" % c)
+            for t in range(PACK):
+                first_layer(c, t, acc[:, t, :])
+            nc.scalar.activation(
+                out=h_bf[:], in_=acc[:].rearrange("p t v -> p v t"), func=GELU, bias=gelu_bias[:]
+            )
             h_q.append(quantize("h%d" % c, h_bf[:].rearrange("p v j -> p (v j)"), CH))
 
         def second_layer(c, a, dst):
@@ -252,7 +236,7 @@ def tile_picked_edgeup_gelu_e_kernel(
         out_rows = out.rearrange("(a p) v -> p a v", p=P)
         for c in range(CHUNKS - 1):
             cols = slice(c * CH, (c + 1) * CH)
-            res = psum.tile([P, 2, CH], F32, name="res%d" % c, tag=("spare", "bank0", "bank1")[c])
+            res = psum.tile([P, 2, CH], F32, name="res%d" % c, tag=("bank0", "bank1", "spare")[c])
             for a in range(2):
                 second_layer(c, a, res[:, a, :])
             res_sb = sb("res_sb%d" % c, [P, 2, CH], F32)
@@ -261,7 +245,7 @@ def tile_picked_edgeup_gelu_e_kernel(
         c = CHUNKS - 1
         cols = slice(c * CH, (c + 1) * CH)
         for a in range(2):
-            res = psum.tile([P, CH], F32, name="res_last%d" % a, tag="bank%d" % (2 + a))
+            res = psum.tile([P, CH], F32, name="res_last%d" % a, tag=("bank2", "acc0")[a])
             second_layer(c, a, res[:])
             res_sb = sb("res_last_sb%d" % a, [P, CH], F32)
             copy_on(("vector", "scalar")[a], res_sb[:], res[:])

@@ -117,10 +117,12 @@ def tile_picked_edgeup_gelu_e_kernel(
         round_pairs("vector", 0, 1536, 1536, 1888)
         round_pairs("scalar", 0, 1536, 1888, 2048)
         gather(0)
-        round_pairs("scalar", 1, 0, 0, 1024)
-        round_pairs("vector", 1, 1024, 1024, 1792)
-        round_pairs("vector", 1, 1792, 1792, 1920)
-        round_pairs("scalar", 1, 1792, 1920, 2048)
+        round_pairs("scalar", 1, 0, 0, 896)
+        round_pairs("vector", 1, 0, 896, 1024)
+        round_pairs("vector", 1, 1024, 1024, 1600)
+        round_pairs("scalar", 1, 1024, 1600, 1792)
+        round_pairs("vector", 1, 1792, 1792, 1968)
+        round_pairs("scalar", 1, 1792, 1968, 2048)
         gather(1)
         x_q = [
             quantize("x%d" % s, picked[s][:].rearrange("p v u -> p (v u)").bitcast(BF16), V)
@@ -172,25 +174,26 @@ def tile_picked_edgeup_gelu_e_kernel(
         cd, sc = quantize("w0", w_flat(0), H)
         for t in range(PACK):
             w_q[0, t] = (cd[:, t * P : (t + 1) * P], sc[:, t * P : (t + 1) * P])
-        warm_up((cd, sc), x_q[0], V)
+        warm_up((cd, sc), x_q[1], V // 2)
         round_weight("scalar", 1, 0, 0, 76)
         round_weight("vector", 1, 0, 76, 128)
         cd, sc = quantize("w1", w_flat(1), H)
         for t in range(PACK):
             w_q[1, t] = (cd[:, t * P : (t + 1) * P], sc[:, t * P : (t + 1) * P])
-        warm_up((cd, sc), x_q[1], V)
-        round_weight("scalar", 2, 0, 0, 58)
-        round_weight("vector", 2, 0, 58, 128)
+        warm_up((cd, sc), x_q[0], V // 2)
+        round_weight("scalar", 2, 0, 0, 46)
+        round_weight("vector", 2, 0, 46, 128)
         round_edges("vector", 0)
         for half in range(2):
             cd, sc = quantize("w2_%d" % half, w_flat(2)[:, half * 1024 : (half + 1) * 1024], 2 * P)
             for t in range(2):
                 w_q[2, 2 * half + t] = (cd[:, t * P : (t + 1) * P], sc[:, t * P : (t + 1) * P])
             if half == 0:
-                warm_up((cd, sc), x_q[1], V // 2)
                 quantize_edges(0)
-        for c in (1, 2, 3):
-            round_edges("scalar" if c == 1 else "vector", c)
+                round_edges("scalar", 1)
+                quantize_edges(1)
+        for c in (2, 3):
+            round_edges("scalar" if c == 2 else "vector", c)
             quantize_edges(c)
 
         def first_layer(c, t, dst):
@@ -212,14 +215,25 @@ def tile_picked_edgeup_gelu_e_kernel(
                 )
 
         h_q = []
-        for c in range(CHUNKS):
+        def hidden(c):
             h_bf = sb("h_bf%d" % c, [P, CH, PACK], BF16)
-            acc = psum.tile([P, PACK, CH], F32, name="acc%d" % c)
-            for t in range(PACK):
-                first_layer(c, t, acc[:, t, :])
-            nc.scalar.activation(
-                out=h_bf[:], in_=acc[:].rearrange("p t v -> p v t"), func=GELU, bias=gelu_bias[:]
-            )
+            if c == 0:
+                h_planes = sb("h_planes", [P, PACK, CH], BF16, tag="e_raw2")
+                for t in range(PACK):
+                    acc_t = psum.tile([P, CH], F32, name="acc0_%d" % t, tag="bank%d" % t)
+                    first_layer(c, t, acc_t[:])
+                    nc.scalar.activation(out=h_planes[:, t, :], in_=acc_t[:], func=GELU, bias=gelu_bias[:])
+                nc.vector.tensor_copy(
+                    out=h_bf[:].rearrange("p (g i) t -> p g t i", i=4),
+                    in_=h_planes[:].rearrange("p t (g i) -> p g t i", i=4),
+                )
+            else:
+                acc = psum.tile([P, PACK, CH], F32, name="acc%d" % c)
+                for t in range(PACK):
+                    first_layer(c, t, acc[:, t, :])
+                nc.scalar.activation(
+                    out=h_bf[:], in_=acc[:].rearrange("p t v -> p v t"), func=GELU, bias=gelu_bias[:]
+                )
             h_q.append(quantize("h%d" % c, h_bf[:].rearrange("p v j -> p (v j)"), CH))
 
         def second_layer(c, a, dst):
@@ -234,18 +248,27 @@ def tile_picked_edgeup_gelu_e_kernel(
             )
 
         out_rows = out.rearrange("(a p) v -> p a v", p=P)
-        for c in range(CHUNKS - 1):
+
+        def way_out(c, engine):
             cols = slice(c * CH, (c + 1) * CH)
-            res = psum.tile([P, 2, CH], F32, name="res%d" % c, tag=("bank0", "bank1", "spare")[c])
+            res = psum.tile([P, 2, CH], F32, name="res%d" % c, tag=("spare", "bank0", "bank1")[c])
             for a in range(2):
                 second_layer(c, a, res[:, a, :])
             res_sb = sb("res_sb%d" % c, [P, 2, CH], F32)
-            copy_on("vector" if c == 0 else "scalar", res_sb[:], res[:])
+            copy_on(engine, res_sb[:], res[:])
             nc.sync.dma_start(out=out_rows[:, :, cols], in_=res_sb[:])
+
+        hidden(0)
+        hidden(1)
+        hidden(2)
+        way_out(0, "vector")
+        hidden(3)
+        way_out(1, "vector")
+        way_out(2, "scalar")
         c = CHUNKS - 1
         cols = slice(c * CH, (c + 1) * CH)
         for a in range(2):
-            res = psum.tile([P, CH], F32, name="res_last%d" % a, tag=("bank2", "acc0")[a])
+            res = psum.tile([P, CH], F32, name="res_last%d" % a, tag="bank%d" % (2 + a))
             second_layer(c, a, res[:])
             res_sb = sb("res_last_sb%d" % a, [P, CH], F32)
             copy_on(("vector", "scalar")[a], res_sb[:], res[:])

@@ -142,19 +142,6 @@ def tile_picked_edgeup_gelu_e_kernel(
         def w_flat(i):
             return w_bf[i][:].rearrange("p t m j -> p (t m j)")
 
-        warm = psum.tile([P, V], F32, name="warm", tag="spare")
-
-        def warm_up(stationary, moving, width):
-            nc.tensor.matmul_mx(
-                out=warm[:, 0:width],
-                lhsT=stationary[0][:, 0:P].bitcast(FP8X4),
-                lhsT_scale=stationary[1][:, 0:P],
-                rhs=moving[0][:, 0:width].bitcast(FP8X4),
-                rhs_scale=moving[1][:, 0:width],
-                start=True,
-                stop=True,
-            )
-
         e_bf = [sb("e_bf%d" % c, [P, CH, PACK], BF16) for c in range(CHUNKS)]
         e_q = {}
 
@@ -168,19 +155,16 @@ def tile_picked_edgeup_gelu_e_kernel(
         def quantize_edges(c):
             e_q[c] = quantize("e%d" % c, e_bf[c][:].rearrange("p v j -> p (v j)"), CH)
 
-        warm_up(x_q[1], x_q[1], V)
         round_weight("scalar", 0, 0, 0, 128)
         w_q = {}
         cd, sc = quantize("w0", w_flat(0), H)
         for t in range(PACK):
             w_q[0, t] = (cd[:, t * P : (t + 1) * P], sc[:, t * P : (t + 1) * P])
-        warm_up((cd, sc), x_q[1], V // 2)
         round_weight("scalar", 1, 0, 0, 76)
         round_weight("vector", 1, 0, 76, 128)
         cd, sc = quantize("w1", w_flat(1), H)
         for t in range(PACK):
             w_q[1, t] = (cd[:, t * P : (t + 1) * P], sc[:, t * P : (t + 1) * P])
-        warm_up((cd, sc), x_q[0], V // 2)
         round_weight("scalar", 2, 0, 0, 46)
         round_weight("vector", 2, 0, 46, 128)
         round_edges("vector", 0)

@@ -13,11 +13,13 @@ U16 = mybir.dt.uint16
 U8 = mybir.dt.uint8
 FP8X4 = mybir.dt.float8_e4m3fn_x4
 GELU = mybir.ActivationFunctionType.Gelu_apprx_tanh
+COPY = mybir.ActivationFunctionType.Copy
 
 P = 128
 PACK = 4
 CH = 128
 CHUNKS = V // CH
+W_ON_SCALAR = (0, 56, 44)
 
 
 def tile_picked_edgeup_gelu_e_kernel(
@@ -37,11 +39,25 @@ def tile_picked_edgeup_gelu_e_kernel(
             else:
                 nc.scalar.copy(out=dst, in_=src)
 
-        def quantize(name, src, width):
-            codes = sb(name + "_codes", [P, width], U32)
+        def quantize(name, src, width, tag=None):
+            codes = sb(name + "_codes", [P, width], U32, tag)
             scales = sb(name + "_scales", [P, width], U8)
             nc.vector.quantize_mx(out=codes[:].bitcast(FP8X4), scales=scales[:], in_=src)
             return codes, scales
+
+        def product(dst, stationary, moving, start, stop):
+            nc.tensor.matmul_mx(
+                out=dst,
+                lhsT=stationary[0].bitcast(FP8X4),
+                lhsT_scale=stationary[1],
+                rhs=moving[0].bitcast(FP8X4),
+                rhs_scale=moving[1],
+                start=start,
+                stop=stop,
+            )
+
+        def columns(pair, i):
+            return pair[0][:, i * P : (i + 1) * P], pair[1][:, i * P : (i + 1) * P]
 
         zero = sb("zero", [P, 1], F32)
         nc.vector.memset(zero[:], 0.0)
@@ -57,203 +73,108 @@ def tile_picked_edgeup_gelu_e_kernel(
             )
 
         x_rows = xT.rearrange("(p j) t -> p j t", j=PACK)
-        x_cuts = ((0, 1536, 2048), (0, 1024, 1792, 2048))
-        x_raw = {}
         offsets = keep.tile([P, 2 * V // 16], U16, name="offsets")
-        for u in range(2):
-            for a, b in zip(x_cuts[u][:-1], x_cuts[u][1:]):
-                x_raw[u, a] = sb("x_raw%d_%d" % (u, a), [P, 2, b - a], F32)
-                nc.sync.dma_start(out=x_raw[u, a][:], in_=x_rows[:, 2 * u : 2 * u + 2, a:b])
-                if u == 0 and a == 0:
-                    nc.sync.dma_start(offsets[:], offs)
-        w_cuts = ((0, 128), (0, 128), (0, 128))
-        w_raw = {}
-        e_raw = {}
+        x_raw = []
+        for j in range(PACK):
+            x_raw.append(sb("x_raw%d" % j, [P, T], F32))
+            nc.sync.dma_start(out=x_raw[j][:], in_=x_rows[:, j, :])
+            if j == 0:
+                nc.sync.dma_start(offsets[:], offs)
+        w_raw = []
+        for i, w in enumerate((w1, w2, w3)):
+            w_raw.append(sb("w_raw%d" % i, [P, PACK, H], F32))
+            nc.sync.dma_start(out=w_raw[i][:], in_=w.rearrange("(p j) c -> p j c", j=PACK))
         e_rows = eT.rearrange("(p j) v -> p j v", j=PACK)
-        w4_cd = sb("w4_cd", [P, N], U32)
-
-        def load_weight(i, piece):
-            m0, m1 = w_cuts[i][piece], w_cuts[i][piece + 1]
-            w_rows = (w1, w2, w3)[i].rearrange("(p j) c -> p j c", j=PACK)
-            w_raw[i, m0] = sb("w_raw%d_%d" % (i, m0), [P, PACK, PACK * (m1 - m0)], F32)
-            nc.sync.dma_start(out=w_raw[i, m0][:], in_=w_rows[:, :, PACK * m0 : PACK * m1])
-
-        def load_edges(c):
-            e_raw[c] = sb("e_raw%d" % c, [P, PACK, CH], F32)
+        e_raw = []
+        for c in range(CHUNKS):
+            e_raw.append(sb("e_raw%d" % c, [P, PACK, CH], F32))
             nc.sync.dma_start(out=e_raw[c][:], in_=e_rows[:, :, c * CH : (c + 1) * CH])
-
-        load_weight(0, 0)
-        load_weight(1, 0)
-        load_weight(2, 0)
-        load_edges(0)
-        load_edges(1)
-        load_edges(2)
-        load_edges(3)
+        w4_cd = sb("w4_cd", [P, N], U32)
         nc.sync.dma_start(
             out=w4_cd[:].bitcast(I32),
             in_=w4_words[0].rearrange("p n r -> p (n r)").bitcast(I32),
         )
 
-        pairs = [sb("pairs%d" % u, [P, T, 2], BF16) for u in range(2)]
-        picked = [sb("picked%d" % s, [P, V, 2], U32) for s in range(2)]
+        src_bf = sb("src_bf", [P, V, PACK], BF16)
+        dst_rows = sb("dst_rows", [P, PACK, V], BF16)
+        dst_bf = sb("dst_bf", [P, V, PACK], BF16)
+        for j in range(PACK):
+            nc.vector.tensor_copy(out=src_bf[:, :, j], in_=x_raw[j][:].indirect(offsets[:, : V // 16]))
+            nc.scalar.activation(dst_rows[:, j, :], x_raw[j][:].indirect(offsets[:, V // 16 :]), COPY)
 
-        def round_pairs(engine, u, start, a, b):
+        def interleave(engine, dst, src, a, b):
             copy_on(
                 engine,
-                pairs[u][:, a:b, :],
-                x_raw[u, start][:, :, a - start : b - start].rearrange("p e t -> p t e"),
+                dst[:, a:b, :].rearrange("p (g i) j -> p g j i", i=4),
+                src[:, :, a:b].rearrange("p j (g i) -> p g j i", i=4),
             )
 
-        def gather(u):
-            window = pairs[u][:].rearrange("p t e -> p (t e)").bitcast(U32)
-            for s in range(2):
-                nc.vector.tensor_copy(
-                    out=picked[s][:, :, u],
-                    in_=window.indirect(offsets[:, s * V // 16 : (s + 1) * V // 16]),
-                )
-
-        round_pairs("vector", 0, 0, 0, 1024)
-        round_pairs("scalar", 0, 0, 1024, 1536)
-        round_pairs("vector", 0, 1536, 1536, 1888)
-        round_pairs("scalar", 0, 1536, 1888, 2048)
-        gather(0)
-        round_pairs("scalar", 1, 0, 0, 896)
-        round_pairs("vector", 1, 0, 896, 1024)
-        round_pairs("vector", 1, 1024, 1024, 1600)
-        round_pairs("scalar", 1, 1024, 1600, 1792)
-        round_pairs("vector", 1, 1792, 1792, 1968)
-        round_pairs("scalar", 1, 1792, 1968, 2048)
-        gather(1)
-        x_q = [
-            quantize("x%d" % s, picked[s][:].rearrange("p v u -> p (v u)").bitcast(BF16), V)
-            for s in range(2)
-        ]
+        src_q = quantize("src", src_bf[:].rearrange("p v j -> p (v j)"), V)
+        interleave("scalar", dst_bf, dst_rows, 0, V)
 
         w_bf = [sb("w_bf%d" % i, [P, PACK, P, PACK], BF16) for i in range(3)]
 
-        def round_weight(engine, i, start, m0, m1):
-            src = w_raw[i, start][:].rearrange("p j (m t) -> p m j t", t=PACK)
-            copy_on(
-                engine,
-                w_bf[i][:].rearrange("p t m j -> p m j t")[:, m0:m1],
-                src[:, m0 - start : m1 - start],
-            )
+        def round_weight(i):
+            src = w_raw[i][:].rearrange("p j (m t) -> p m j t", t=PACK)
+            dst = w_bf[i][:].rearrange("p t m j -> p m j t")
+            m = W_ON_SCALAR[i]
+            if m:
+                copy_on("scalar", dst[:, :m], src[:, :m])
+            copy_on("vector", dst[:, m:], src[:, m:])
 
         def w_flat(i):
             return w_bf[i][:].rearrange("p t m j -> p (t m j)")
 
-        e_bf = [sb("e_bf%d" % c, [P, CH, PACK], BF16) for c in range(CHUNKS)]
-        e_q = {}
+        acc = [psum.tile([P, PACK, CH], F32, name="acc%d" % c) for c in range(CHUNKS)]
 
-        def round_edges(engine, c):
-            copy_on(
-                engine,
-                e_bf[c][:].rearrange("p (g i) j -> p g j i", i=4),
-                e_raw[c][:].rearrange("p j (g i) -> p g j i", i=4),
-            )
-
-        def quantize_edges(c):
-            e_q[c] = quantize("e%d" % c, e_bf[c][:].rearrange("p v j -> p (v j)"), CH)
-
-        round_weight("scalar", 0, 0, 0, 128)
-        w_q = {}
-        cd, sc = quantize("w0", w_flat(0), H)
-        for t in range(PACK):
-            w_q[0, t] = (cd[:, t * P : (t + 1) * P], sc[:, t * P : (t + 1) * P])
-        round_weight("scalar", 1, 0, 0, 76)
-        round_weight("vector", 1, 0, 76, 128)
-        cd, sc = quantize("w1", w_flat(1), H)
-        for t in range(PACK):
-            w_q[1, t] = (cd[:, t * P : (t + 1) * P], sc[:, t * P : (t + 1) * P])
-        round_weight("scalar", 2, 0, 0, 46)
-        round_weight("vector", 2, 0, 46, 128)
-        round_edges("vector", 0)
-        for half in range(2):
-            cd, sc = quantize("w2_%d" % half, w_flat(2)[:, half * 1024 : (half + 1) * 1024], 2 * P)
-            for t in range(2):
-                w_q[2, 2 * half + t] = (cd[:, t * P : (t + 1) * P], sc[:, t * P : (t + 1) * P])
-            if half == 0:
-                quantize_edges(0)
-                round_edges("scalar", 1)
-                quantize_edges(1)
-        for c in (2, 3):
-            round_edges("scalar" if c == 2 else "vector", c)
-            quantize_edges(c)
-
-        def first_layer(c, t, dst):
-            cols = slice(c * CH, (c + 1) * CH)
-            moving = [
-                (x_q[0][0][:, cols], x_q[0][1][:, cols]),
-                (x_q[1][0][:, cols], x_q[1][1][:, cols]),
-                (e_q[c][0][:], e_q[c][1][:]),
-            ]
-            for i in range(3):
-                nc.tensor.matmul_mx(
-                    out=dst,
-                    lhsT=w_q[i, t][0].bitcast(FP8X4),
-                    lhsT_scale=w_q[i, t][1],
-                    rhs=moving[i][0].bitcast(FP8X4),
-                    rhs_scale=moving[i][1],
-                    start=(i == 0),
-                    stop=(i == 2),
-                )
-
-        h_q = []
-        def hidden(c):
-            h_bf = sb("h_bf%d" % c, [P, CH, PACK], BF16)
-            if c == 0:
-                h_planes = sb("h_planes", [P, PACK, CH], BF16, tag="e_raw2")
-                for t in range(PACK):
-                    acc_t = psum.tile([P, CH], F32, name="acc0_%d" % t, tag="bank%d" % t)
-                    first_layer(c, t, acc_t[:])
-                    nc.scalar.activation(out=h_planes[:, t, :], in_=acc_t[:], func=GELU, bias=gelu_bias[:])
-                nc.vector.tensor_copy(
-                    out=h_bf[:].rearrange("p (g i) t -> p g t i", i=4),
-                    in_=h_planes[:].rearrange("p t (g i) -> p g t i", i=4),
-                )
-            else:
-                acc = psum.tile([P, PACK, CH], F32, name="acc%d" % c)
-                for t in range(PACK):
-                    first_layer(c, t, acc[:, t, :])
-                nc.scalar.activation(
-                    out=h_bf[:], in_=acc[:].rearrange("p t v -> p v t"), func=GELU, bias=gelu_bias[:]
-                )
-            h_q.append(quantize("h%d" % c, h_bf[:].rearrange("p v j -> p (v j)"), CH))
-
-        def second_layer(c, a, dst):
-            nc.tensor.matmul_mx(
-                out=dst,
-                lhsT=w4_cd[:, a * P : (a + 1) * P].bitcast(FP8X4),
-                lhsT_scale=w4_sc[:, a * P : (a + 1) * P],
-                rhs=h_q[c][0][:].bitcast(FP8X4),
-                rhs_scale=h_q[c][1][:],
-                start=True,
-                stop=True,
-            )
+        round_weight(0)
+        w1_q = quantize("w1", w_flat(0), H)
+        for c in range(CHUNKS):
+            for t in range(PACK):
+                product(acc[c][:, t, :], columns(w1_q, t), columns(src_q, c), t == 0, False)
+        dst_q = quantize("dst", dst_bf[:].rearrange("p v j -> p (v j)"), V, "w_raw0")
+        round_weight(1)
+        w2_q = quantize("w2", w_flat(1), H)
+        for c in range(CHUNKS):
+            for t in range(PACK):
+                product(acc[c][:, t, :], columns(w2_q, t), columns(dst_q, c), False, False)
+        round_weight(2)
+        w3_q = [quantize("w3_%d" % u, w_flat(2)[:, u * 1024 : (u + 1) * 1024], 2 * P) for u in range(2)]
 
         out_rows = out.rearrange("(a p) v -> p a v", p=P)
+        h_q = []
+
+        def hidden(c, engine):
+            e_bf = sb("e_bf%d" % c, [P, CH, PACK], BF16)
+            interleave(engine, e_bf, e_raw[c], 0, CH)
+            e_q = quantize("e%d" % c, e_bf[:].rearrange("p v j -> p (v j)"), CH)
+            for t in range(PACK):
+                product(acc[c][:, t, :], columns(w3_q[t // 2], t % 2), columns(e_q, 0), False, t == PACK - 1)
+            h_bf = sb("h_bf%d" % c, [P, CH, PACK], BF16)
+            nc.scalar.activation(
+                out=h_bf[:], in_=acc[c][:].rearrange("p t v -> p v t"), func=GELU, bias=gelu_bias[:]
+            )
+            h_q.append(quantize("h%d" % c, h_bf[:].rearrange("p v j -> p (v j)"), CH))
 
         def way_out(c, engine):
-            cols = slice(c * CH, (c + 1) * CH)
-            res = psum.tile([P, 2, CH], F32, name="res%d" % c, tag=("spare", "bank0", "bank1")[c])
+            res = psum.tile([P, 2, CH], F32, name="res%d" % c)
             for a in range(2):
-                second_layer(c, a, res[:, a, :])
+                product(res[:, a, :], columns((w4_cd, w4_sc), a), columns(h_q[c], 0), True, True)
             res_sb = sb("res_sb%d" % c, [P, 2, CH], F32)
             copy_on(engine, res_sb[:], res[:])
-            nc.sync.dma_start(out=out_rows[:, :, cols], in_=res_sb[:])
+            nc.sync.dma_start(out=out_rows[:, :, c * CH : (c + 1) * CH], in_=res_sb[:])
 
-        hidden(0)
-        hidden(1)
-        hidden(2)
+        hidden(0, "scalar")
+        hidden(1, "scalar")
+        hidden(2, "vector")
         way_out(0, "vector")
-        hidden(3)
+        hidden(3, "vector")
         way_out(1, "vector")
-        way_out(2, "scalar")
+        way_out(2, "vector")
         c = CHUNKS - 1
-        cols = slice(c * CH, (c + 1) * CH)
-        for a in range(2):
-            res = psum.tile([P, CH], F32, name="res_last%d" % a, tag="bank%d" % (2 + a))
-            second_layer(c, a, res[:])
+        for a, engine in enumerate(("vector", "scalar")):
+            res = psum.tile([P, CH], F32, name="res_last%d" % a, tag=("res_last", "acc0")[a])
+            product(res[:], columns((w4_cd, w4_sc), a), columns(h_q[c], 0), True, True)
             res_sb = sb("res_last_sb%d" % a, [P, CH], F32)
-            copy_on(("vector", "scalar")[a], res_sb[:], res[:])
-            (nc.sync, nc.scalar)[a].dma_start(out=out_rows[:, a, cols], in_=res_sb[:])
+            copy_on(engine, res_sb[:], res[:])
+            (nc.sync, nc.scalar)[a].dma_start(out=out_rows[:, a, c * CH : (c + 1) * CH], in_=res_sb[:])

@@ -19,7 +19,8 @@ P = 128
 PACK = 4
 CH = 128
 CHUNKS = V // CH
-W_ON_SCALAR = (0, 56, 44)
+W2_ON_SCALAR = 56
+W3_ON_SCALAR = (36, 22)
 
 
 def tile_picked_edgeup_gelu_e_kernel(
@@ -81,12 +82,17 @@ def tile_picked_edgeup_gelu_e_kernel(
             if j == 0:
                 nc.sync.dma_start(offsets[:], offs)
         w_raw = []
-        for i, w in enumerate((w1, w2, w3)):
+        for i, w in enumerate((w1, w2)):
             w_raw.append(sb("w_raw%d" % i, [P, PACK, H], F32))
             nc.sync.dma_start(out=w_raw[i][:], in_=w.rearrange("(p j) c -> p j c", j=PACK))
         e_rows = eT.rearrange("(p j) v -> p j v", j=PACK)
+        w3_rows = w3.rearrange("(p j) c -> p j c", j=PACK)
         e_raw = []
+        w3_raw = []
         for c in range(CHUNKS):
+            if c < 2:
+                w3_raw.append(sb("w3_raw%d" % c, [P, PACK, H // 2], F32))
+                nc.sync.dma_start(out=w3_raw[c][:], in_=w3_rows[:, :, c * H // 2 : (c + 1) * H // 2])
             e_raw.append(sb("e_raw%d" % c, [P, PACK, CH], F32))
             nc.sync.dma_start(out=e_raw[c][:], in_=e_rows[:, :, c * CH : (c + 1) * CH])
         w4_cd = sb("w4_cd", [P, N], U32)
@@ -99,7 +105,12 @@ def tile_picked_edgeup_gelu_e_kernel(
         dst_rows = sb("dst_rows", [P, PACK, V], BF16)
         dst_bf = sb("dst_bf", [P, V, PACK], BF16)
         for j in range(PACK):
-            nc.vector.tensor_copy(out=src_bf[:, :, j], in_=x_raw[j][:].indirect(offsets[:, : V // 16]))
+            pieces = 2 if j == PACK - 1 else 1
+            n = V // pieces
+            for a in range(0, V, n):
+                nc.vector.tensor_copy(
+                    out=src_bf[:, a : a + n, j], in_=x_raw[j][:].indirect(offsets[:, a // 16 : (a + n) // 16])
+                )
             nc.scalar.activation(dst_rows[:, j, :], x_raw[j][:].indirect(offsets[:, V // 16 :]), COPY)
 
         def interleave(engine, dst, src, a, b):
@@ -109,47 +120,67 @@ def tile_picked_edgeup_gelu_e_kernel(
                 src[:, :, a:b].rearrange("p j (g i) -> p g j i", i=4),
             )
 
-        src_q = quantize("src", src_bf[:].rearrange("p v j -> p (v j)"), V)
+        src_q = [
+            quantize("src%d" % u, src_bf[:, u * 2 * CH : (u + 1) * 2 * CH, :].rearrange("p v j -> p (v j)"), 2 * CH)
+            for u in range(2)
+        ]
         interleave("scalar", dst_bf, dst_rows, 0, V)
 
-        w_bf = [sb("w_bf%d" % i, [P, PACK, P, PACK], BF16) for i in range(3)]
+        w_bf = [sb("w_bf%d" % i, [P, PACK, P, PACK], BF16) for i in range(2)]
 
-        def round_weight(i):
-            src = w_raw[i][:].rearrange("p j (m t) -> p m j t", t=PACK)
-            dst = w_bf[i][:].rearrange("p t m j -> p m j t")
-            m = W_ON_SCALAR[i]
-            if m:
-                copy_on("scalar", dst[:, :m], src[:, :m])
-            copy_on("vector", dst[:, m:], src[:, m:])
+        def round_weight(bf, raw, m):
+            src = raw[:].rearrange("p j (m t) -> p m j t", t=PACK)
+            dst = bf[:].rearrange("p t m j -> p m j t")
+            for t in (0, 2):
+                if m:
+                    copy_on("scalar", dst[:, :m, :, t : t + 2], src[:, :m, :, t : t + 2])
+                copy_on("vector", dst[:, m:, :, t : t + 2], src[:, m:, :, t : t + 2])
 
-        def w_flat(i):
-            return w_bf[i][:].rearrange("p t m j -> p (t m j)")
+        def quantize_weight(i):
+            return [
+                quantize("w%d_%d" % (i, u), w_bf[i][:, 2 * u : 2 * u + 2].rearrange("p t m j -> p (t m j)"), 2 * P)
+                for u in range(2)
+            ]
 
         acc = [psum.tile([P, PACK, CH], F32, name="acc%d" % c) for c in range(CHUNKS)]
 
-        round_weight(0)
-        w1_q = quantize("w1", w_flat(0), H)
-        for c in range(CHUNKS):
-            for t in range(PACK):
-                product(acc[c][:, t, :], columns(w1_q, t), columns(src_q, c), t == 0, False)
+        round_weight(w_bf[0], w_raw[0], 0)
+        w1_q = quantize_weight(0)
+        for t in range(PACK):
+            for c in range(CHUNKS):
+                product(acc[c][:, t, :], columns(w1_q[t // 2], t % 2), columns(src_q[c // 2], c % 2), t == 0, False)
         dst_q = quantize("dst", dst_bf[:].rearrange("p v j -> p (v j)"), V, "w_raw0")
-        round_weight(1)
-        w2_q = quantize("w2", w_flat(1), H)
-        for c in range(CHUNKS):
+        round_weight(w_bf[1], w_raw[1], W2_ON_SCALAR)
+        w2_q = quantize_weight(1)
+        for t in range(PACK):
+            for c in range(CHUNKS):
+                product(acc[c][:, t, :], columns(w2_q[t // 2], t % 2), columns(dst_q, c), False, False)
+        w3_q = (sb("w3_codes", [P, H], U32), sb("w3_scales", [P, H], U8))
+
+        def third_weight(u):
+            bf = sb("w3_bf%d" % u, [P, PACK, P // 2, PACK], BF16)
+            round_weight(bf, w3_raw[u], W3_ON_SCALAR[u])
             for t in range(PACK):
-                product(acc[c][:, t, :], columns(w2_q, t), columns(dst_q, c), False, False)
-        round_weight(2)
-        w3_q = [quantize("w3_%d" % u, w_flat(2)[:, u * 1024 : (u + 1) * 1024], 2 * P) for u in range(2)]
+                cols = slice(t * P + u * P // 2, t * P + (u + 1) * P // 2)
+                nc.vector.quantize_mx(
+                    out=w3_q[0][:, cols].bitcast(FP8X4),
+                    scales=w3_q[1][:, cols],
+                    in_=bf[:, t].rearrange("p m j -> p (m j)"),
+                )
 
         out_rows = out.rearrange("(a p) v -> p a v", p=P)
         h_q = []
 
-        def hidden(c, engine):
+        e_q = []
+
+        def edges(c, engine):
             e_bf = sb("e_bf%d" % c, [P, CH, PACK], BF16)
             interleave(engine, e_bf, e_raw[c], 0, CH)
-            e_q = quantize("e%d" % c, e_bf[:].rearrange("p v j -> p (v j)"), CH)
+            e_q.append(quantize("e%d" % c, e_bf[:].rearrange("p v j -> p (v j)"), CH))
+
+        def hidden(c):
             for t in range(PACK):
-                product(acc[c][:, t, :], columns(w3_q[t // 2], t % 2), columns(e_q, 0), False, t == PACK - 1)
+                product(acc[c][:, t, :], columns(w3_q, t), columns(e_q[c], 0), False, t == PACK - 1)
             h_bf = sb("h_bf%d" % c, [P, CH, PACK], BF16)
             nc.scalar.activation(
                 out=h_bf[:], in_=acc[c][:].rearrange("p t v -> p v t"), func=GELU, bias=gelu_bias[:]
@@ -164,11 +195,17 @@ def tile_picked_edgeup_gelu_e_kernel(
             copy_on(engine, res_sb[:], res[:])
             nc.sync.dma_start(out=out_rows[:, :, c * CH : (c + 1) * CH], in_=res_sb[:])
 
-        hidden(0, "scalar")
-        hidden(1, "scalar")
-        hidden(2, "vector")
+        third_weight(0)
+        edges(0, "scalar")
+        third_weight(1)
+        hidden(0)
+        edges(1, "scalar")
+        hidden(1)
+        edges(2, "vector")
+        hidden(2)
         way_out(0, "vector")
-        hidden(3, "vector")
+        edges(3, "vector")
+        hidden(3)
         way_out(1, "vector")
         way_out(2, "vector")
         c = CHUNKS - 1

@@ -19,6 +19,7 @@ P = 128
 PACK = 4
 CH = 128
 CHUNKS = V // CH
+E2_ON_SCALAR = 76
 W2_ON_SCALAR = 56
 W3_ON_SCALAR = (36, 22)
 
@@ -60,18 +61,18 @@ def tile_picked_edgeup_gelu_e_kernel(
         def columns(pair, i):
             return pair[0][:, i * P : (i + 1) * P], pair[1][:, i * P : (i + 1) * P]
 
-        zero = sb("zero", [P, 1], F32)
-        nc.vector.memset(zero[:], 0.0)
-        gelu_bias = sb("gelu_bias", [P, 1], F32)
-        nc.scalar.activation(out=gelu_bias[:], in_=zero[:], func=GELU)
-
         w4_sc = sb("w4_sc", [P, N], U8)
-        nc.vector.memset(w4_sc[:].bitcast(I32), 0)
+        nc.gpsimd.memset(w4_sc[:].bitcast(I32), 0)
         for q in range(4):
             nc.scalar.dma_start(
                 out=w4_sc[32 * q : 32 * q + 4, :].bitcast(I32),
                 in_=w4_scales[0, 4 * q : 4 * q + 4, :].bitcast(I32),
             )
+
+        zero = sb("zero", [P, 1], F32)
+        nc.vector.memset(zero[:], 0.0)
+        gelu_bias = sb("gelu_bias", [P, 1], F32)
+        nc.scalar.activation(out=gelu_bias[:], in_=zero[:], func=GELU)
 
         x_rows = xT.rearrange("(p j) t -> p j t", j=PACK)
         offsets = keep.tile([P, 2 * V // 16], U16, name="offsets")
@@ -170,48 +171,57 @@ def tile_picked_edgeup_gelu_e_kernel(
 
         out_rows = out.rearrange("(a p) v -> p a v", p=P)
         h_q = []
+        h_bf = []
 
         e_q = []
 
-        def edges(c, engine):
+        def edges(c, on_scalar):
             e_bf = sb("e_bf%d" % c, [P, CH, PACK], BF16)
-            interleave(engine, e_bf, e_raw[c], 0, CH)
+            if on_scalar:
+                interleave("scalar", e_bf, e_raw[c], 0, on_scalar)
+            if on_scalar < CH:
+                interleave("vector", e_bf, e_raw[c], on_scalar, CH)
             e_q.append(quantize("e%d" % c, e_bf[:].rearrange("p v j -> p (v j)"), CH))
 
         def hidden(c):
             for t in range(PACK):
                 product(acc[c][:, t, :], columns(w3_q, t), columns(e_q[c], 0), False, t == PACK - 1)
-            h_bf = sb("h_bf%d" % c, [P, CH, PACK], BF16)
+            h_bf.append(sb("h_bf%d" % c, [P, CH, PACK], BF16, "e_raw2" if c == 0 else None))
             nc.scalar.activation(
-                out=h_bf[:], in_=acc[c][:].rearrange("p t v -> p v t"), func=GELU, bias=gelu_bias[:]
+                out=h_bf[c][:], in_=acc[c][:].rearrange("p t v -> p v t"), func=GELU,
+                bias=gelu_bias[:] if c == 0 else 0.0,
             )
-            h_q.append(quantize("h%d" % c, h_bf[:].rearrange("p v j -> p (v j)"), CH))
 
-        def way_out(c, engine):
+        def quantize_hidden(c, tag=None):
+            h_q.append(quantize("h%d" % c, h_bf[c][:].rearrange("p v j -> p (v j)"), CH, tag))
+
+        def way_out(c, engine, tag=None):
             res = psum.tile([P, 2, CH], F32, name="res%d" % c)
             for a in range(2):
                 product(res[:, a, :], columns((w4_cd, w4_sc), a), columns(h_q[c], 0), True, True)
-            res_sb = sb("res_sb%d" % c, [P, 2, CH], F32)
+            res_sb = sb("res_sb%d" % c, [P, 2, CH], F32, tag)
             copy_on(engine, res_sb[:], res[:])
             nc.sync.dma_start(out=out_rows[:, :, c * CH : (c + 1) * CH], in_=res_sb[:])
 
         third_weight(0)
-        edges(0, "scalar")
+        edges(0, CH)
         third_weight(1)
-        hidden(0)
-        edges(1, "scalar")
-        hidden(1)
-        edges(2, "vector")
-        hidden(2)
-        way_out(0, "vector")
-        edges(3, "vector")
-        hidden(3)
+        edges(1, CH)
+        edges(2, E2_ON_SCALAR)
+        edges(3, 0)
+        for c in range(CHUNKS):
+            hidden(c)
+        quantize_hidden(0)
+        quantize_hidden(1)
+        way_out(0, "vector", "h_bf1")
+        quantize_hidden(2)
         way_out(1, "vector")
-        way_out(2, "vector")
+        quantize_hidden(3)
+        way_out(2, "scalar")
         c = CHUNKS - 1
+        res_sb = sb("res_last_sb", [P, 2, CH], F32)
         for a, engine in enumerate(("vector", "scalar")):
             res = psum.tile([P, CH], F32, name="res_last%d" % a, tag=("res_last", "acc0")[a])
             product(res[:], columns((w4_cd, w4_sc), a), columns(h_q[c], 0), True, True)
-            res_sb = sb("res_last_sb%d" % a, [P, CH], F32)
-            copy_on(engine, res_sb[:], res[:])
-            (nc.sync, nc.scalar)[a].dma_start(out=out_rows[:, a, c * CH : (c + 1) * CH], in_=res_sb[:])
+            copy_on(engine, res_sb[:, a, :], res[:])
+        nc.sync.dma_start(out=out_rows[:, :, c * CH : (c + 1) * CH], in_=res_sb[:])

@@ -137,25 +137,14 @@ def tile_picked_edgeup_gelu_e_kernel(
                     copy_on("scalar", dst[:, :m, :, t : t + 2], src[:, :m, :, t : t + 2])
                 copy_on("vector", dst[:, m:, :, t : t + 2], src[:, m:, :, t : t + 2])
 
-        def quantize_weight(i):
+        def quantize_weight(i, tags=(None, None)):
             return [
-                quantize("w%d_%d" % (i, u), w_bf[i][:, 2 * u : 2 * u + 2].rearrange("p t m j -> p (t m j)"), 2 * P)
+                quantize(
+                    "w%d_%d" % (i, u), w_bf[i][:, 2 * u : 2 * u + 2].rearrange("p t m j -> p (t m j)"), 2 * P, tags[u]
+                )
                 for u in range(2)
             ]
 
-        acc = [psum.tile([P, PACK, CH], F32, name="acc%d" % c) for c in range(CHUNKS)]
-
-        round_weight(w_bf[0], w_raw[0], 0)
-        w1_q = quantize_weight(0)
-        for t in range(PACK):
-            for c in range(CHUNKS):
-                product(acc[c][:, t, :], columns(w1_q[t // 2], t % 2), columns(src_q[c // 2], c % 2), t == 0, False)
-        dst_q = quantize("dst", dst_bf[:].rearrange("p v j -> p (v j)"), V, "w_raw0")
-        round_weight(w_bf[1], w_raw[1], W2_ON_SCALAR)
-        w2_q = quantize_weight(1)
-        for t in range(PACK):
-            for c in range(CHUNKS):
-                product(acc[c][:, t, :], columns(w2_q[t // 2], t % 2), columns(dst_q, c), False, False)
         w3_q = (sb("w3_codes", [P, H], U32), sb("w3_scales", [P, H], U8))
 
         def third_weight(u):
@@ -169,10 +158,6 @@ def tile_picked_edgeup_gelu_e_kernel(
                     in_=bf[:, t].rearrange("p m j -> p (m j)"),
                 )
 
-        out_rows = out.rearrange("(a p) v -> p a v", p=P)
-        h_q = []
-        h_bf = []
-
         e_q = []
 
         def edges(c, on_scalar):
@@ -182,6 +167,26 @@ def tile_picked_edgeup_gelu_e_kernel(
             if on_scalar < CH:
                 interleave("vector", e_bf, e_raw[c], on_scalar, CH)
             e_q.append(quantize("e%d" % c, e_bf[:].rearrange("p v j -> p (v j)"), CH))
+
+        acc = [psum.tile([P, PACK, CH], F32, name="acc%d" % c) for c in range(CHUNKS)]
+
+        round_weight(w_bf[0], w_raw[0], 0)
+        w1_q = quantize_weight(0)
+        for t in range(PACK):
+            for c in range(CHUNKS):
+                product(acc[c][:, t, :], columns(w1_q[t // 2], t % 2), columns(src_q[c // 2], c % 2), t == 0, False)
+        dst_q = quantize("dst", dst_bf[:].rearrange("p v j -> p (v j)"), V, "w_raw0")
+        round_weight(w_bf[1], w_raw[1], W2_ON_SCALAR)
+        third_weight(0)
+        edges(0, CH)
+        w2_q = quantize_weight(1, (None, "e_raw0"))
+        for t in range(PACK):
+            for c in range(CHUNKS):
+                product(acc[c][:, t, :], columns(w2_q[t // 2], t % 2), columns(dst_q, c), False, False)
+
+        out_rows = out.rearrange("(a p) v -> p a v", p=P)
+        h_q = []
+        h_bf = []
 
         def hidden(c):
             for t in range(PACK):
@@ -203,8 +208,6 @@ def tile_picked_edgeup_gelu_e_kernel(
             copy_on(engine, res_sb[:], res[:])
             nc.sync.dma_start(out=out_rows[:, :, c * CH : (c + 1) * CH], in_=res_sb[:])
 
-        third_weight(0)
-        edges(0, CH)
         third_weight(1)
         edges(1, CH)
         edges(2, E2_ON_SCALAR)

@@ -19,9 +19,9 @@ P = 128
 PACK = 4
 CH = 128
 CHUNKS = V // CH
-E2_ON_SCALAR = 76
+E2_ON_SCALAR = 64
 W2_ON_SCALAR = 56
-W3_ON_SCALAR = (36, 22)
+W3_ON_SCALAR = (32, 22)
 
 
 def tile_picked_edgeup_gelu_e_kernel(
@@ -179,7 +179,7 @@ def tile_picked_edgeup_gelu_e_kernel(
         round_weight(w_bf[1], w_raw[1], W2_ON_SCALAR)
         third_weight(0)
         edges(0, CH)
-        w2_q = quantize_weight(1, (None, "e_raw0"))
+        w2_q = quantize_weight(1, (None, "w3_bf0"))
         for t in range(PACK):
             for c in range(CHUNKS):
                 product(acc[c][:, t, :], columns(w2_q[t // 2], t % 2), columns(dst_q, c), False, False)

@@ -19,6 +19,7 @@ P = 128
 PACK = 4
 CH = 128
 CHUNKS = V // CH
+E1_ON_SCALAR = 96
 E2_ON_SCALAR = 64
 W2_ON_SCALAR = 56
 W3_ON_SCALAR = (32, 22)
@@ -209,7 +210,7 @@ def tile_picked_edgeup_gelu_e_kernel(
             nc.sync.dma_start(out=out_rows[:, :, c * CH : (c + 1) * CH], in_=res_sb[:])
 
         third_weight(1)
-        edges(1, CH)
+        edges(1, E1_ON_SCALAR)
         edges(2, E2_ON_SCALAR)
         edges(3, 0)
         for c in range(CHUNKS):

@@ -34,7 +34,7 @@ def tile_picked_edgeup_gelu_e_kernel(
         psum = ctx.enter_context(tc.psum_pool(name="psum", bufs=1))
 
         def sb(name, shape, dtype, tag=None):
-            return keep.tile(shape, dtype, name=name, tag=tag or name, align_bytes=64)
+            return keep.tile(shape, dtype, name=name, tag=tag or name, align_bytes=256)
 
         def copy_on(engine, dst, src):
             if engine == "vector":

@@ -34,7 +34,9 @@ def tile_picked_edgeup_gelu_e_kernel(
         psum = ctx.enter_context(tc.psum_pool(name="psum", bufs=1))
 
         def sb(name, shape, dtype, tag=None):
-            return keep.tile(shape, dtype, name=name, tag=tag or name, align_bytes=256)
+            tag = tag or name
+            moved_by_dma = "_raw" in tag or tag in ("w4_cd", "h_bf1") or tag.startswith("res")
+            return keep.tile(shape, dtype, name=name, tag=tag, align_bytes=2048 if moved_by_dma else 256)
 
         def copy_on(engine, dst, src):
             if engine == "vector":
@@ -76,7 +78,7 @@ def tile_picked_edgeup_gelu_e_kernel(
         nc.scalar.activation(out=gelu_bias[:], in_=zero[:], func=GELU)
 
         x_rows = xT.rearrange("(p j) t -> p j t", j=PACK)
-        offsets = keep.tile([P, 2 * V // 16], U16, name="offsets")
+        offsets = keep.tile([P, 2 * V // 16], U16, name="offsets", align_bytes=256)
         x_raw = []
         for j in range(PACK):
             x_raw.append(sb("x_raw%d" % j, [P, T], F32))

@@ -21,7 +21,7 @@ CH = 128
 CHUNKS = V // CH
 E1_ON_SCALAR = 96
 E2_ON_SCALAR = 64
-W2_ON_SCALAR = 56
+W2_ON_SCALAR = 52
 W3_ON_SCALAR = (32, 22)
 
 
@@ -106,7 +106,7 @@ def tile_picked_edgeup_gelu_e_kernel(
         )
 
         src_bf = sb("src_bf", [P, V, PACK], BF16)
-        dst_rows = sb("dst_rows", [P, PACK, V], BF16)
+        dst_rows = [sb("dst_rows%d" % u, [P, 2, V], BF16) for u in range(2)]
         dst_bf = sb("dst_bf", [P, V, PACK], BF16)
         for j in range(PACK):
             pieces = 2 if j == PACK - 1 else 1
@@ -115,7 +115,9 @@ def tile_picked_edgeup_gelu_e_kernel(
                 nc.vector.tensor_copy(
                     out=src_bf[:, a : a + n, j], in_=x_raw[j][:].indirect(offsets[:, a // 16 : (a + n) // 16])
                 )
-            nc.scalar.activation(dst_rows[:, j, :], x_raw[j][:].indirect(offsets[:, V // 16 :]), COPY)
+            nc.scalar.activation(dst_rows[j // 2][:, j % 2, :], x_raw[j][:].indirect(offsets[:, V // 16 :]), COPY)
+            if j == 1:
+                copy_on("scalar", dst_bf[:, :, 0:2], dst_rows[0][:].rearrange("p j v -> p v j"))
 
         def interleave(engine, dst, src, a, b):
             copy_on(
@@ -128,7 +130,7 @@ def tile_picked_edgeup_gelu_e_kernel(
             quantize("src%d" % u, src_bf[:, u * 2 * CH : (u + 1) * 2 * CH, :].rearrange("p v j -> p (v j)"), 2 * CH)
             for u in range(2)
         ]
-        interleave("scalar", dst_bf, dst_rows, 0, V)
+        copy_on("scalar", dst_bf[:, :, 2:4], dst_rows[1][:].rearrange("p j v -> p v j"))
 
         w_bf = [sb("w_bf%d" % i, [P, PACK, P, PACK], BF16) for i in range(2)]
 
@@ -182,7 +184,7 @@ def tile_picked_edgeup_gelu_e_kernel(
         round_weight(w_bf[1], w_raw[1], W2_ON_SCALAR)
         third_weight(0)
         edges(0, CH)
-        w2_q = quantize_weight(1, (None, "w3_bf0"))
+        w2_q = quantize_weight(1, (None, "w3_raw0"))
         for t in range(PACK):
             for c in range(CHUNKS):
                 product(acc[c][:, t, :], columns(w2_q[t // 2], t % 2), columns(dst_q, c), False, False)

@@ -21,8 +21,10 @@ CH = 128
 CHUNKS = V // CH
 E1_ON_SCALAR = 96
 E2_ON_SCALAR = 64
-W2_ON_SCALAR = 52
-W3_ON_SCALAR = (32, 22)
+W1_ON_SCALAR = (0, 32)
+W2_ON_SCALAR = (52, 52)
+W3_ON_SCALAR = ((32, 32), (22, 22))
+H0_BEYOND = PACK * CH // 2 - (CH - E2_ON_SCALAR)
 
 
 def tile_picked_edgeup_gelu_e_kernel(
@@ -97,7 +99,11 @@ def tile_picked_edgeup_gelu_e_kernel(
             if c < 2:
                 w3_raw.append(sb("w3_raw%d" % c, [P, PACK, H // 2], F32))
                 nc.sync.dma_start(out=w3_raw[c][:], in_=w3_rows[:, :, c * H // 2 : (c + 1) * H // 2])
-            e_raw.append(sb("e_raw%d" % c, [P, PACK, CH], F32))
+            if c == 2:
+                e2_raw_h0 = sb("e_raw2", [P, PACK * CH + H0_BEYOND], F32)
+                e_raw.append(e2_raw_h0[:, : PACK * CH].rearrange("p (j v) -> p j v", j=PACK))
+            else:
+                e_raw.append(sb("e_raw%d" % c, [P, PACK, CH], F32))
             nc.sync.dma_start(out=e_raw[c][:], in_=e_rows[:, :, c * CH : (c + 1) * CH])
         w4_cd = sb("w4_cd", [P, N], U32)
         nc.sync.dma_start(
@@ -115,7 +121,11 @@ def tile_picked_edgeup_gelu_e_kernel(
                 nc.vector.tensor_copy(
                     out=src_bf[:, a : a + n, j], in_=x_raw[j][:].indirect(offsets[:, a // 16 : (a + n) // 16])
                 )
-            nc.scalar.activation(dst_rows[j // 2][:, j % 2, :], x_raw[j][:].indirect(offsets[:, V // 16 :]), COPY)
+                nc.scalar.activation(
+                    dst_rows[j // 2][:, j % 2, a : a + n],
+                    x_raw[j][:].indirect(offsets[:, (V + a) // 16 : (V + a + n) // 16]),
+                    COPY,
+                )
             if j == 1:
                 copy_on("scalar", dst_bf[:, :, 0:2], dst_rows[0][:].rearrange("p j v -> p v j"))
 
@@ -130,14 +140,17 @@ def tile_picked_edgeup_gelu_e_kernel(
             quantize("src%d" % u, src_bf[:, u * 2 * CH : (u + 1) * 2 * CH, :].rearrange("p v j -> p (v j)"), 2 * CH)
             for u in range(2)
         ]
-        copy_on("scalar", dst_bf[:, :, 2:4], dst_rows[1][:].rearrange("p j v -> p v j"))
+        for a in range(0, V, V // 2):
+            copy_on(
+                "scalar", dst_bf[:, a : a + V // 2, 2:4], dst_rows[1][:, :, a : a + V // 2].rearrange("p j v -> p v j")
+            )
 
         w_bf = [sb("w_bf%d" % i, [P, PACK, P, PACK], BF16) for i in range(2)]
 
-        def round_weight(bf, raw, m):
+        def round_weight(bf, raw, shares):
             src = raw[:].rearrange("p j (m t) -> p m j t", t=PACK)
             dst = bf[:].rearrange("p t m j -> p m j t")
-            for t in (0, 2):
+            for t, m in zip((0, 2), shares):
                 if m:
                     copy_on("scalar", dst[:, :m, :, t : t + 2], src[:, :m, :, t : t + 2])
                 copy_on("vector", dst[:, m:, :, t : t + 2], src[:, m:, :, t : t + 2])
@@ -175,7 +188,7 @@ def tile_picked_edgeup_gelu_e_kernel(
 
         acc = [psum.tile([P, PACK, CH], F32, name="acc%d" % c) for c in range(CHUNKS)]
 
-        round_weight(w_bf[0], w_raw[0], 0)
+        round_weight(w_bf[0], w_raw[0], W1_ON_SCALAR)
         w1_q = quantize_weight(0)
         for t in range(PACK):
             for c in range(CHUNKS):
@@ -196,7 +209,10 @@ def tile_picked_edgeup_gelu_e_kernel(
         def hidden(c):
             for t in range(PACK):
                 product(acc[c][:, t, :], columns(w3_q, t), columns(e_q[c], 0), False, t == PACK - 1)
-            h_bf.append(sb("h_bf%d" % c, [P, CH, PACK], BF16, "e_raw2" if c == 0 else None))
+            if c == 0:
+                h_bf.append(e2_raw_h0[:, (PACK - 1) * CH + E2_ON_SCALAR :].bitcast(BF16).rearrange("p (v j) -> p v j", j=PACK))
+            else:
+                h_bf.append(sb("h_bf%d" % c, [P, CH, PACK], BF16))
             nc.scalar.activation(
                 out=h_bf[c][:], in_=acc[c][:].rearrange("p t v -> p v t"), func=GELU,
                 bias=gelu_bias[:] if c == 0 else 0.0,

@@ -21,7 +21,7 @@ CH = 128
 CHUNKS = V // CH
 E1_ON_SCALAR = 96
 E2_ON_SCALAR = 64
-W1_ON_SCALAR = (0, 32)
+W1_ON_SCALAR = (0, 16)
 W2_ON_SCALAR = (52, 52)
 W3_ON_SCALAR = ((32, 32), (22, 22))
 H0_BEYOND = PACK * CH // 2 - (CH - E2_ON_SCALAR)
@@ -127,7 +127,12 @@ def tile_picked_edgeup_gelu_e_kernel(
                     COPY,
                 )
             if j == 1:
-                copy_on("scalar", dst_bf[:, :, 0:2], dst_rows[0][:].rearrange("p j v -> p v j"))
+                for a, engine in ((0, "vector"), (V // 2, "scalar")):
+                    copy_on(
+                        engine,
+                        dst_bf[:, a : a + V // 2, 0:2],
+                        dst_rows[0][:, :, a : a + V // 2].rearrange("p j v -> p v j"),
+                    )
 
         def interleave(engine, dst, src, a, b):
             copy_on(

@@ -37,7 +37,7 @@ def tile_picked_edgeup_gelu_e_kernel(
 
         def sb(name, shape, dtype, tag=None):
             tag = tag or name
-            moved_by_dma = "_raw" in tag or tag in ("w4_cd", "h_bf1") or tag.startswith("res")
+            moved_by_dma = "_raw" in tag or tag in ("w4_cd", "zero", "e3_codes") or tag.startswith("res")
             return keep.tile(shape, dtype, name=name, tag=tag, align_bytes=2048 if moved_by_dma else 256)
 
         def copy_on(engine, dst, src):
@@ -220,7 +220,7 @@ def tile_picked_edgeup_gelu_e_kernel(
                 h_bf.append(sb("h_bf%d" % c, [P, CH, PACK], BF16))
             nc.scalar.activation(
                 out=h_bf[c][:], in_=acc[c][:].rearrange("p t v -> p v t"), func=GELU,
-                bias=gelu_bias[:] if c == 0 else 0.0,
+                bias=(gelu_bias[:], 0.0, zero[:], 0.0)[c],
             )
 
         def quantize_hidden(c, tag=None):
@@ -242,10 +242,10 @@ def tile_picked_edgeup_gelu_e_kernel(
             hidden(c)
         quantize_hidden(0)
         quantize_hidden(1)
-        way_out(0, "vector", "h_bf1")
         quantize_hidden(2)
-        way_out(1, "vector")
+        way_out(0, "vector", "zero")
         quantize_hidden(3)
+        way_out(1, "scalar", "e3_codes")
         way_out(2, "scalar")
         c = CHUNKS - 1
         res_sb = sb("res_last_sb", [P, 2, CH], F32)

@@ -218,10 +218,14 @@ def tile_picked_edgeup_gelu_e_kernel(
                 h_bf.append(e2_raw_h0[:, (PACK - 1) * CH + E2_ON_SCALAR :].bitcast(BF16).rearrange("p (v j) -> p v j", j=PACK))
             else:
                 h_bf.append(sb("h_bf%d" % c, [P, CH, PACK], BF16))
-            nc.scalar.activation(
-                out=h_bf[c][:], in_=acc[c][:].rearrange("p t v -> p v t"), func=GELU,
-                bias=(gelu_bias[:], 0.0, zero[:], 0.0)[c],
-            )
+            pieces = 2 if c == CHUNKS - 1 else 1
+            for a in range(0, CH, CH // pieces):
+                nc.scalar.activation(
+                    out=h_bf[c][:, a : a + CH // pieces, :],
+                    in_=acc[c][:, :, a : a + CH // pieces].rearrange("p t v -> p v t"),
+                    func=GELU,
+                    bias=(gelu_bias[:], 0.0, zero[:], 0.0)[c],
+                )
 
         def quantize_hidden(c, tag=None):
             h_q.append(quantize("h%d" % c, h_bf[c][:].rearrange("p v j -> p (v j)"), CH, tag))
@@ -237,14 +241,28 @@ def tile_picked_edgeup_gelu_e_kernel(
         third_weight(1)
         edges(1, E1_ON_SCALAR)
         edges(2, E2_ON_SCALAR)
-        edges(3, 0)
+        last_bf = [sb("e_bf3_%d" % u, [P, CH // 2, PACK], BF16) for u in range(2)]
+        for u in range(2):
+            interleave("vector", last_bf[u], e_raw[3][:, :, u * CH // 2 : (u + 1) * CH // 2], 0, CH // 2)
+        e_q.append((sb("e3_codes", [P, CH], U32), sb("e3_scales", [P, CH], U8)))
+        for u in range(2):
+            cols = slice(u * CH // 2, (u + 1) * CH // 2)
+            nc.vector.quantize_mx(
+                out=e_q[3][0][:, cols].bitcast(FP8X4), scales=e_q[3][1][:, cols], in_=last_bf[u][:].rearrange("p v j -> p (v j)")
+            )
         for c in range(CHUNKS):
             hidden(c)
-        quantize_hidden(0)
+        quantize_hidden(0, "e_raw3")
         quantize_hidden(1)
         quantize_hidden(2)
         way_out(0, "vector", "zero")
-        quantize_hidden(3)
+        h_q.append((sb("h3_codes", [P, CH], U32), sb("h3_scales", [P, CH], U8)))
+        for a in range(0, CH, CH // 2):
+            nc.vector.quantize_mx(
+                out=h_q[3][0][:, a : a + CH // 2].bitcast(FP8X4),
+                scales=h_q[3][1][:, a : a + CH // 2],
+                in_=h_bf[3][:, a : a + CH // 2, :].rearrange("p v j -> p (v j)"),
+            )
         way_out(1, "scalar", "e3_codes")
         way_out(2, "scalar")
         c = CHUNKS - 1

@@ -224,7 +224,7 @@ def tile_picked_edgeup_gelu_e_kernel(
                     out=h_bf[c][:, a : a + CH // pieces, :],
                     in_=acc[c][:, :, a : a + CH // pieces].rearrange("p t v -> p v t"),
                     func=GELU,
-                    bias=(gelu_bias[:], 0.0, zero[:], 0.0)[c],
+                    bias=gelu_bias[:] if c == 0 else 0.0,
                 )
 
         def quantize_hidden(c, tag=None):
@@ -254,8 +254,8 @@ def tile_picked_edgeup_gelu_e_kernel(
             hidden(c)
         quantize_hidden(0, "e_raw3")
         quantize_hidden(1)
+        way_out(0, "vector")
         quantize_hidden(2)
-        way_out(0, "vector", "zero")
         h_q.append((sb("h3_codes", [P, CH], U32), sb("h3_scales", [P, CH], U8)))
         for a in range(0, CH, CH // 2):
             nc.vector.quantize_mx(
@@ -264,11 +264,10 @@ def tile_picked_edgeup_gelu_e_kernel(
                 in_=h_bf[3][:, a : a + CH // 2, :].rearrange("p v j -> p (v j)"),
             )
         way_out(1, "scalar", "e3_codes")
-        way_out(2, "scalar")
-        c = CHUNKS - 1
-        res_sb = sb("res_last_sb", [P, 2, CH], F32)
-        for a, engine in enumerate(("vector", "scalar")):
-            res = psum.tile([P, CH], F32, name="res_last%d" % a, tag=("res_last", "acc0")[a])
-            product(res[:], columns((w4_cd, w4_sc), a), columns(h_q[c], 0), True, True)
-            copy_on(engine, res_sb[:, a, :], res[:])
-        nc.sync.dma_start(out=out_rows[:, :, c * CH : (c + 1) * CH], in_=res_sb[:])
+        for c, banks in ((2, ("res2", "acc1")), (3, ("res_last", "acc0"))):
+            res_sb = sb("res_sb%d" % c, [P, 2, CH], F32)
+            for a, engine in enumerate(("vector", "scalar")):
+                res = psum.tile([P, CH], F32, name="res%d_%d" % (c, a), tag=banks[a])
+                product(res[:], columns((w4_cd, w4_sc), a), columns(h_q[c], 0), True, True)
+                copy_on(engine, res_sb[:, a, :], res[:])
+            nc.sync.dma_start(out=out_rows[:, :, c * CH : (c + 1) * CH], in_=res_sb[:])

from contextlib import ExitStack

import concourse.mybir as mybir

K, T, V, H, N = 512, 2048, 512, 512, 256
FLOPS = 2 * V * (3 * K * H + H * N)

F32 = mybir.dt.float32
BF16 = mybir.dt.bfloat16
U32 = mybir.dt.uint32
I32 = mybir.dt.int32
U16 = mybir.dt.uint16
U8 = mybir.dt.uint8
FP8X4 = mybir.dt.float8_e4m3fn_x4
GELU = mybir.ActivationFunctionType.Gelu_apprx_tanh
COPY = mybir.ActivationFunctionType.Copy

P = 128
PACK = 4
CH = 128
CHUNKS = V // CH
E1_ON_SCALAR = 96
E2_ON_SCALAR = 64
W1_ON_SCALAR = (0, 16)
W2_ON_SCALAR = (52, 52)
W3_ON_SCALAR = ((32, 32), (22, 22))
H0_BEYOND = PACK * CH // 2 - (CH - E2_ON_SCALAR)


def tile_picked_edgeup_gelu_e_kernel(
    tc, xT, eT, w1, w2, w3, w4_words, w4_scales, offs, out
):
    nc = tc.nc
    with ExitStack() as ctx:
        keep = ctx.enter_context(tc.tile_pool(name="keep", bufs=1))
        psum = ctx.enter_context(tc.psum_pool(name="psum", bufs=1))

        def sb(name, shape, dtype, tag=None):
            tag = tag or name
            moved_by_dma = "_raw" in tag or tag in ("w4_cd", "zero", "e3_codes") or tag.startswith("res")
            return keep.tile(shape, dtype, name=name, tag=tag, align_bytes=2048 if moved_by_dma else 256)

        def copy_on(engine, dst, src):
            if engine == "vector":
                nc.vector.tensor_copy(out=dst, in_=src)
            else:
                nc.scalar.copy(out=dst, in_=src)

        def quantize(name, src, width, tag=None):
            codes = sb(name + "_codes", [P, width], U32, tag)
            scales = sb(name + "_scales", [P, width], U8)
            nc.vector.quantize_mx(out=codes[:].bitcast(FP8X4), scales=scales[:], in_=src)
            return codes, scales

        def product(dst, stationary, moving, start, stop):
            nc.tensor.matmul_mx(
                out=dst,
                lhsT=stationary[0].bitcast(FP8X4),
                lhsT_scale=stationary[1],
                rhs=moving[0].bitcast(FP8X4),
                rhs_scale=moving[1],
                start=start,
                stop=stop,
            )

        def columns(pair, i):
            return pair[0][:, i * P : (i + 1) * P], pair[1][:, i * P : (i + 1) * P]

        w4_sc = sb("w4_sc", [P, N], U8)
        nc.gpsimd.memset(w4_sc[:].bitcast(I32), 0)
        for q in range(4):
            nc.scalar.dma_start(
                out=w4_sc[32 * q : 32 * q + 4, :].bitcast(I32),
                in_=w4_scales[0, 4 * q : 4 * q + 4, :].bitcast(I32),
            )

        zero = sb("zero", [P, 1], F32)
        nc.vector.memset(zero[:], 0.0)
        gelu_bias = sb("gelu_bias", [P, 1], F32)
        nc.scalar.activation(out=gelu_bias[:], in_=zero[:], func=GELU)

        x_rows = xT.rearrange("(p j) t -> p j t", j=PACK)
        offsets = keep.tile([P, 2 * V // 16], U16, name="offsets", align_bytes=256)
        x_raw = []
        for j in range(PACK):
            x_raw.append(sb("x_raw%d" % j, [P, T], F32))
            nc.sync.dma_start(out=x_raw[j][:], in_=x_rows[:, j, :])
            if j == 0:
                nc.sync.dma_start(offsets[:], offs)
        w_raw = []
        for i, w in enumerate((w1, w2)):
            w_raw.append(sb("w_raw%d" % i, [P, PACK, H], F32))
            nc.sync.dma_start(out=w_raw[i][:], in_=w.rearrange("(p j) c -> p j c", j=PACK))
        e_rows = eT.rearrange("(p j) v -> p j v", j=PACK)
        w3_rows = w3.rearrange("(p j) c -> p j c", j=PACK)
        e_raw = []
        w3_raw = []
        for c in range(CHUNKS):
            if c < 2:
                w3_raw.append(sb("w3_raw%d" % c, [P, PACK, H // 2], F32))
                nc.sync.dma_start(out=w3_raw[c][:], in_=w3_rows[:, :, c * H // 2 : (c + 1) * H // 2])
            if c == 2:
                e2_raw_h0 = sb("e_raw2", [P, PACK * CH + H0_BEYOND], F32)
                e_raw.append(e2_raw_h0[:, : PACK * CH].rearrange("p (j v) -> p j v", j=PACK))
            else:
                e_raw.append(sb("e_raw%d" % c, [P, PACK, CH], F32))
            nc.sync.dma_start(out=e_raw[c][:], in_=e_rows[:, :, c * CH : (c + 1) * CH])
        w4_cd = sb("w4_cd", [P, N], U32)
        nc.sync.dma_start(
            out=w4_cd[:].bitcast(I32),
            in_=w4_words[0].rearrange("p n r -> p (n r)").bitcast(I32),
        )

        src_bf = sb("src_bf", [P, V, PACK], BF16)
        dst_rows = [sb("dst_rows%d" % u, [P, 2, V], BF16) for u in range(2)]
        dst_bf = sb("dst_bf", [P, V, PACK], BF16)
        for j in range(PACK):
            pieces = 2 if j == PACK - 1 else 1
            n = V // pieces
            for a in range(0, V, n):
                nc.vector.tensor_copy(
                    out=src_bf[:, a : a + n, j], in_=x_raw[j][:].indirect(offsets[:, a // 16 : (a + n) // 16])
                )
                nc.scalar.activation(
                    dst_rows[j // 2][:, j % 2, a : a + n],
                    x_raw[j][:].indirect(offsets[:, (V + a) // 16 : (V + a + n) // 16]),
                    COPY,
                )
            if j == 1:
                for a, engine in ((0, "vector"), (V // 2, "scalar")):
                    copy_on(
                        engine,
                        dst_bf[:, a : a + V // 2, 0:2],
                        dst_rows[0][:, :, a : a + V // 2].rearrange("p j v -> p v j"),
                    )

        def interleave(engine, dst, src, a, b):
            copy_on(
                engine,
                dst[:, a:b, :].rearrange("p (g i) j -> p g j i", i=4),
                src[:, :, a:b].rearrange("p j (g i) -> p g j i", i=4),
            )

        src_q = [
            quantize("src%d" % u, src_bf[:, u * 2 * CH : (u + 1) * 2 * CH, :].rearrange("p v j -> p (v j)"), 2 * CH)
            for u in range(2)
        ]
        for a in range(0, V, V // 2):
            copy_on(
                "scalar", dst_bf[:, a : a + V // 2, 2:4], dst_rows[1][:, :, a : a + V // 2].rearrange("p j v -> p v j")
            )

        w_bf = [sb("w_bf%d" % i, [P, PACK, P, PACK], BF16) for i in range(2)]

        def round_weight(bf, raw, shares):
            src = raw[:].rearrange("p j (m t) -> p m j t", t=PACK)
            dst = bf[:].rearrange("p t m j -> p m j t")
            for t, m in zip((0, 2), shares):
                if m:
                    copy_on("scalar", dst[:, :m, :, t : t + 2], src[:, :m, :, t : t + 2])
                copy_on("vector", dst[:, m:, :, t : t + 2], src[:, m:, :, t : t + 2])

        def quantize_weight(i, tags=(None, None)):
            return [
                quantize(
                    "w%d_%d" % (i, u), w_bf[i][:, 2 * u : 2 * u + 2].rearrange("p t m j -> p (t m j)"), 2 * P, tags[u]
                )
                for u in range(2)
            ]

        w3_q = (sb("w3_codes", [P, H], U32), sb("w3_scales", [P, H], U8))

        def third_weight(u):
            bf = sb("w3_bf%d" % u, [P, PACK, P // 2, PACK], BF16)
            round_weight(bf, w3_raw[u], W3_ON_SCALAR[u])
            for t in range(PACK):
                cols = slice(t * P + u * P // 2, t * P + (u + 1) * P // 2)
                nc.vector.quantize_mx(
                    out=w3_q[0][:, cols].bitcast(FP8X4),
                    scales=w3_q[1][:, cols],
                    in_=bf[:, t].rearrange("p m j -> p (m j)"),
                )

        e_q = []

        def edges(c, on_scalar):
            e_bf = sb("e_bf%d" % c, [P, CH, PACK], BF16)
            if on_scalar:
                interleave("scalar", e_bf, e_raw[c], 0, on_scalar)
            if on_scalar < CH:
                interleave("vector", e_bf, e_raw[c], on_scalar, CH)
            e_q.append(quantize("e%d" % c, e_bf[:].rearrange("p v j -> p (v j)"), CH))

        acc = [psum.tile([P, PACK, CH], F32, name="acc%d" % c) for c in range(CHUNKS)]

        round_weight(w_bf[0], w_raw[0], W1_ON_SCALAR)
        w1_q = quantize_weight(0)
        for t in range(PACK):
            for c in range(CHUNKS):
                product(acc[c][:, t, :], columns(w1_q[t // 2], t % 2), columns(src_q[c // 2], c % 2), t == 0, False)
        dst_q = quantize("dst", dst_bf[:].rearrange("p v j -> p (v j)"), V, "w_raw0")
        round_weight(w_bf[1], w_raw[1], W2_ON_SCALAR)
        third_weight(0)
        edges(0, CH)
        w2_q = quantize_weight(1, (None, "w3_raw0"))
        for t in range(PACK):
            for c in range(CHUNKS):
                product(acc[c][:, t, :], columns(w2_q[t // 2], t % 2), columns(dst_q, c), False, False)

        out_rows = out.rearrange("(a p) v -> p a v", p=P)
        h_q = []
        h_bf = []

        def hidden(c):
            for t in range(PACK):
                product(acc[c][:, t, :], columns(w3_q, t), columns(e_q[c], 0), False, t == PACK - 1)
            if c == 0:
                h_bf.append(e2_raw_h0[:, (PACK - 1) * CH + E2_ON_SCALAR :].bitcast(BF16).rearrange("p (v j) -> p v j", j=PACK))
            else:
                h_bf.append(sb("h_bf%d" % c, [P, CH, PACK], BF16))
            pieces = 2 if c == CHUNKS - 1 else 1
            for a in range(0, CH, CH // pieces):
                nc.scalar.activation(
                    out=h_bf[c][:, a : a + CH // pieces, :],
                    in_=acc[c][:, :, a : a + CH // pieces].rearrange("p t v -> p v t"),
                    func=GELU,
                    bias=gelu_bias[:] if c == 0 else 0.0,
                )

        def quantize_hidden(c, tag=None):
            h_q.append(quantize("h%d" % c, h_bf[c][:].rearrange("p v j -> p (v j)"), CH, tag))

        def way_out(c, engine, tag=None):
            res = psum.tile([P, 2, CH], F32, name="res%d" % c)
            for a in range(2):
                product(res[:, a, :], columns((w4_cd, w4_sc), a), columns(h_q[c], 0), True, True)
            res_sb = sb("res_sb%d" % c, [P, 2, CH], F32, tag)
            copy_on(engine, res_sb[:], res[:])
            nc.sync.dma_start(out=out_rows[:, :, c * CH : (c + 1) * CH], in_=res_sb[:])

        third_weight(1)
        edges(1, E1_ON_SCALAR)
        edges(2, E2_ON_SCALAR)
        last_bf = [sb("e_bf3_%d" % u, [P, CH // 2, PACK], BF16) for u in range(2)]
        for u in range(2):
            interleave("vector", last_bf[u], e_raw[3][:, :, u * CH // 2 : (u + 1) * CH // 2], 0, CH // 2)
        e_q.append((sb("e3_codes", [P, CH], U32), sb("e3_scales", [P, CH], U8)))
        for u in range(2):
            cols = slice(u * CH // 2, (u + 1) * CH // 2)
            nc.vector.quantize_mx(
                out=e_q[3][0][:, cols].bitcast(FP8X4), scales=e_q[3][1][:, cols], in_=last_bf[u][:].rearrange("p v j -> p (v j)")
            )
        for c in range(CHUNKS):
            hidden(c)
        quantize_hidden(0, "e_raw3")
        quantize_hidden(1)
        way_out(0, "vector")
        quantize_hidden(2)
        h_q.append((sb("h3_codes", [P, CH], U32), sb("h3_scales", [P, CH], U8)))
        for a in range(0, CH, CH // 2):
            nc.vector.quantize_mx(
                out=h_q[3][0][:, a : a + CH // 2].bitcast(FP8X4),
                scales=h_q[3][1][:, a : a + CH // 2],
                in_=h_bf[3][:, a : a + CH // 2, :].rearrange("p v j -> p (v j)"),
            )
        way_out(1, "scalar", "e3_codes")
        for c, banks in ((2, ("res2", "acc1")), (3, ("res_last", "acc0"))):
            res_sb = sb("res_sb%d" % c, [P, 2, CH], F32)
            for a, engine in enumerate(("vector", "scalar")):
                res = psum.tile([P, CH], F32, name="res%d_%d" % (c, a), tag=banks[a])
                product(res[:], columns((w4_cd, w4_sc), a), columns(h_q[c], 0), True, True)
                copy_on(engine, res_sb[:, a, :], res[:])
            nc.sync.dma_start(out=out_rows[:, :, c * CH : (c + 1) * CH], in_=res_sb[:])
